import numpy as np
import ml_dtypes


def mxq(x, axis, fmt="e4m3"):
    dtype, down = {"e4m3": (ml_dtypes.float8_e4m3fn, 7), "e5m2": (ml_dtypes.float8_e5m2, 14)}[fmt]
    v = np.moveaxis(np.asarray(x, np.float32).astype(ml_dtypes.bfloat16).astype(np.float64), axis, -1)
    blocks = v.reshape(v.shape[:-1] + (-1, 32))
    amax = np.abs(blocks).max(-1, keepdims=True)
    byte = np.maximum(np.where(amax > 0, np.frexp(amax)[1] - 1 + 127, 0) - down, 1)
    scale = np.exp2(byte - 127.0)
    codes = (blocks / scale).astype(np.float32).astype(dtype).astype(np.float64)
    return np.moveaxis((codes * scale).reshape(v.shape), -1, axis)


WIDE = False


def mx_kscale(k):
    if not WIDE:
        return np.ones(k)
    levels = np.array([10, -10, 5, -5, 0])
    if k % 512:
        return np.exp2(np.random.permutation(np.resize(levels, k // 32))).repeat(32)
    a = np.empty((k // 512, 16))
    for p in range(k // 512):
        a[p, :8] = np.random.permutation(np.resize(levels, 8))
        for g in range(8):
            far = levels[np.abs(levels - a[p, g]) >= 10]
            a[p, g + 8] = far[np.random.randint(len(far))]
    return np.exp2(a.ravel()).repeat(32)


def f64(x):
    return np.asarray(x).astype(np.float64)


def striped(idx):
    return np.tile(idx.reshape(-1, 16).T, (8, 1)).astype(np.uint16)


def unstriped(offs):
    return offs[:16].T.reshape(-1).astype(np.int64)


E2M1 = np.array([0.0, 0.5, 1.0, 1.5, 2.0, 3.0, 4.0, 6.0, -0.0, -0.5, -1.0, -1.5, -2.0, -3.0, -4.0, -6.0])


def pack_weight(w, fmt):
    k, n = w.shape
    w = f64(np.asarray(w, np.float32).astype(ml_dtypes.bfloat16)).reshape(k // 32, 32, n)
    amax = np.abs(w).max(1)
    if fmt == "e4m3":
        byte = np.frexp(amax)[1] - 1 + 127 - 7
    else:
        mant, ex = np.frexp(amax / 6.0)
        byte = np.where(mant > 0.5, ex, ex - 1) + 127
    byte = np.clip(np.where(amax > 0, byte, 1), 1, 254)
    scaled = (w * np.exp2(127.0 - byte)[:, None, :]).reshape(k, n).astype(np.float32)
    by_word = np.ascontiguousarray(scaled.reshape(k // 512, 128, 4, n).transpose(0, 1, 3, 2))
    if fmt == "e4m3":
        words = by_word.astype(ml_dtypes.float8_e4m3fn).view(np.uint8)
    else:
        c = by_word.astype(ml_dtypes.float4_e2m1fn).view(np.uint8) & 0xF
        words = (c[..., 0::2] | (c[..., 1::2] << 4)).reshape(k // 512, 128, 2 * n)
    return np.ascontiguousarray(words), np.ascontiguousarray(byte.astype(np.uint8).reshape(k // 512, 16, n))


def unpack_weight(words, scales, fmt):
    g, _, n = scales.shape
    words = np.ascontiguousarray(words).reshape(g, 128, n, -1)
    if fmt == "e4m3":
        vals = words.view(ml_dtypes.float8_e4m3fn).astype(np.float64)
    else:
        nib = np.empty((g, 128, n, 4), np.uint8)
        nib[..., 0::2] = words & 0xF
        nib[..., 1::2] = words >> 4
        vals = E2M1[nib]
    vals = vals * np.repeat(np.exp2(scales.astype(np.float64) - 127.0), 8, axis=1)[..., None]
    return vals.transpose(0, 1, 3, 2).reshape(g * 512, n)


def relu(v):
    return np.maximum(v, 0.0)


K, T, E, C, H, N = 512, 768, 8, 128, 512, 256
TOP = 4
PAD = 64


def by_expert(wq, xq):
    return np.concatenate([wq[e].T @ xq[:, e * C:(e + 1) * C] for e in range(E)], axis=1)


def setup_inputs():
    n = np.random.standard_normal
    s = mx_kscale(K)[:, None]
    u = mx_kscale(H)
    slot_token = np.empty(E * C, np.int64); pos = np.tile(E * C + np.arange(T) % PAD, (TOP, 1)); taken = np.zeros(T, np.int64)
    liked = np.random.randn(T)
    for e in np.random.permutation(E):
        free = np.flatnonzero(taken < TOP); pick = np.random.permutation(free[np.argsort(-(liked[free] + np.random.gumbel(size=free.size)))[:C]]); slot_token[e * C:(e + 1) * C] = pick
        pos[taken[pick], pick] = e * C + np.arange(C); taken[pick] += 1
    g = np.random.uniform(0.2, 0.8, (TOP, T))
    w1 = [pack_weight(m, "e2m1") for m in n((E, K, H)) / np.sqrt(K) / s[None]]
    w3 = [pack_weight(m, "e2m1") for m in n((E, K, H)) / np.sqrt(K) / s[None] * u[None, None, :]]
    w2 = [pack_weight(m, "e2m1") for m in n((E, H, N)) / np.sqrt(H) / u[None, :, None]]
    return {
        "xT": (n((K, T)) * s).astype(np.float32),
        "w1_words": np.stack([m[0] for m in w1]),
        "w1_scales": np.stack([m[1] for m in w1]),
        "w3_words": np.stack([m[0] for m in w3]),
        "w3_scales": np.stack([m[1] for m in w3]),
        "w2_words": np.stack([m[0] for m in w2]),
        "w2_scales": np.stack([m[1] for m in w2]),
        "gate": np.stack([np.tile(r, (N, 1)) for r in g]).astype(np.float32),
        "offs": striped(slot_token),
        "pos1": striped(pos[0]),
        "pos2": striped(pos[1]),
        "pos3": striped(pos[2]),
        "pos4": striped(pos[3]),
    }


def reference(xT, w1_words, w1_scales, w3_words, w3_scales, w2_words, w2_scales, gate, offs, pos1, pos2, pos3, pos4):
    idx = unstriped(offs)
    w1 = np.stack([unpack_weight(w1_words[e], w1_scales[e], "e2m1") for e in range(E)])
    w3 = np.stack([unpack_weight(w3_words[e], w3_scales[e], "e2m1") for e in range(E)])
    w2 = np.stack([unpack_weight(w2_words[e], w2_scales[e], "e2m1") for e in range(E)])
    xq = mxq(f64(xT)[:, idx], 0, "e4m3")
    h = relu(by_expert(w1, xq))
    h = h * by_expert(w3, xq)
    y = by_expert(w2, mxq(h, 0, "e4m3"))
    y = np.concatenate([y, np.zeros((N, PAD))], axis=1)
    return sum(f64(gate[r]) * y[:, unstriped(p)] for r, p in enumerate((pos1, pos2, pos3, pos4)))

@@ -1,0 +1,255 @@
+from contextlib import ExitStack
+
+import concourse.mybir as mybir
+from concourse.masks import make_identity
+
+K, T, E, C, H, N = 512, 768, 8, 128, 512, 256
+TOP, PAD = 4, 64
+S = E * C
+FLOPS = 2 * S * (2 * K * H + H * N)
+
+F32 = mybir.dt.float32
+BF16 = mybir.dt.bfloat16
+I32 = mybir.dt.int32
+U32 = mybir.dt.uint32
+U16 = mybir.dt.uint16
+U8 = mybir.dt.uint8
+FP8X4 = mybir.dt.float8_e4m3fn_x4
+FP4X4 = mybir.dt.float4_e2m1fn_x4
+MULT = mybir.AluOpType.mult
+ADD = mybir.AluOpType.add
+RELU = mybir.ActivationFunctionType.Relu
+
+P = 128
+X_CHUNK = 256
+X_LAST_VECTOR = 160
+W_GROUPS = [(0, 1), (1, 2), (2, 4), (4, 6), (6, 8)]
+GATHER_GROUPS = {0: (0, 1), 1: (1, 2), 2: (2, 4), 4: (4, 6), 6: (6, 8)}
+Y_GROUPS = [(0, 2), (2, 4), (4, 6), (6, 7), (7, 8)]
+
+
+def tile_moe_ecr_glu_relu_kernel(
+    tc, xT, w1_words, w1_scales, w3_words, w3_scales, w2_words, w2_scales, gate, offs, pos1, pos2, pos3, pos4, out
+):
+    nc = tc.nc
+    with ExitStack() as ctx:
+        keep = ctx.enter_context(tc.tile_pool(name="keep", bufs=1))
+        psum = ctx.enter_context(tc.psum_pool(name="psum", bufs=1))
+
+        def sb(name, shape, dtype):
+            return keep.tile(shape, dtype, name=name, align_bytes=64)
+
+        offs_sb = sb("offs_sb", [P, S // 16], U16)
+        pos_sb = [sb("pos_sb%d" % r, [P, T // 16], U16) for r in range(TOP)]
+        n_chunks = T // X_CHUNK
+        x_raw = [sb("x_raw%d" % c, [P, 4, X_CHUNK], F32) for c in range(n_chunks)]
+        x_bf = [sb("x_bf%d" % c, [P, X_CHUNK, 4], BF16) for c in range(n_chunks)]
+        x_words = sb("x_words", [P, T], U32)
+        x_scales = sb("x_scales", [P, T], U8)
+        g_words = sb("g_words", [P, S], U32)
+        g_scales = sb("g_scales", [P, S], U8)
+        s1 = [sb("s1_%d" % h, [P, 4, H], U8) for h in range(2)]
+        s3 = sb("s3", [P, E, H], U8)
+        s2 = sb("s2", [P, E, N], U8)
+        w1 = [sb("w1_%d" % a, [P, b - a, 2 * H], U8) for a, b in W_GROUPS]
+        w3 = [sb("w3_%d" % a, [P, b - a, 2 * H], U8) for a, b in W_GROUPS]
+        w2 = [sb("w2_%d" % h, [P, 4, 2 * N], U8) for h in range(2)]
+        gate_sb = [[sb("gate%d_%d" % (hf, r), [P, T], F32) for r in range(TOP)] for hf in range(2)]
+        ident = sb("ident", [P, P], F32)
+        warm = sb("warm", [P, 8], F32)
+        relu_a = [sb("relu_a%d" % e, [P, H], F32) for e in range(E)]
+        h_rows = [sb("h_rows%d" % e, [P, H], BF16) for e in range(E)]
+        h_cols = [sb("h_cols%d" % e, [P, H], BF16) for e in range(E)]
+        h_words = [sb("h_words%d" % e, [P, C], U32) for e in range(E)]
+        h_scales = [sb("h_scales%d" % e, [P, C], U8) for e in range(E)]
+        y = [sb("y%d" % hf, [P, S + PAD], F32) for hf in range(2)]
+        prod = [[sb("prod%d_%d" % (hf, r), [P, T], F32) for r in range(TOP)] for hf in range(2)]
+        turned = [sb("turned%d" % hf, [P, T], F32) for hf in range(2)]
+        res = [sb("res%d" % hf, [P, T], F32) for hf in range(2)]
+
+        bank_a = [psum.tile([P, 512], F32, name="bank_a%d" % i) for i in range(2)]
+        bank_b = [psum.tile([P, 512], F32, name="bank_b%d" % i) for i in range(2)]
+        bank_t = [psum.tile([P, 512], F32, name="bank_t%d" % i) for i in range(2)]
+        bank_y = [psum.tile([P, 512], F32, name="bank_y%d" % i) for i in range(2)]
+
+        def zero(t):
+            nc.vector.memset(t[:].rearrange("p e n -> p (e n)").bitcast(I32), 0)
+
+        def load_scales(eng, plane, src, a, b):
+            for r in range(4):
+                eng.dma_start(
+                    out=plane[r:P:32, :, :].bitcast(I32),
+                    in_=src[a:b, 0, r:16:4, :].rearrange("e q n -> q e n").bitcast(I32),
+                )
+
+        def load_words(dst, src, a, b):
+            nc.sync.dma_start(out=dst[:].bitcast(I32), in_=src[a:b, 0].rearrange("e p n -> p e n").bitcast(I32))
+
+        zero(s3)
+        zero(s1[0])
+        zero(s1[1])
+        zero(s2)
+        nc.vector.memset(x_scales[:].bitcast(I32), 0)
+        for hf in range(2):
+            nc.vector.memset(y[hf][:, S:], 0.0)
+        nc.vector.memset(warm[:, 0:4], 0.0)
+        nc.scalar.activation(warm[:, 4:8], warm[:, 0:4], RELU)
+
+        nc.sync.dma_start(offs_sb[:], offs)
+        for c in range(n_chunks):
+            nc.sync.dma_start(
+                out=x_raw[c][:], in_=xT[:, c * X_CHUNK : (c + 1) * X_CHUNK].rearrange("(p j) w -> p j w", j=4)
+            )
+        load_scales(nc.gpsimd, s3, w3_scales, 0, E)
+        load_scales(nc.sync, s1[0], w1_scales, 0, 4)
+        make_identity(nc, ident[:])
+        for g in range(len(W_GROUPS)):
+            if g == 3:
+                load_scales(nc.sync, s1[1], w1_scales, 4, 8)
+            load_words(w1[g], w1_words, *W_GROUPS[g])
+            load_words(w3[g], w3_words, *W_GROUPS[g])
+        load_scales(nc.sync, s2, w2_scales, 0, E)
+        load_words(w2[0], w2_words, 0, 4)
+        load_words(w2[1], w2_words, 4, 8)
+        for r, pos in enumerate((pos1, pos2, pos3, pos4)):
+            nc.sync.dma_start(pos_sb[r][:], pos)
+        for hf in range(2):
+            for r in reversed(range(TOP)):
+                nc.sync.dma_start(out=gate_sb[hf][r][:], in_=gate[r, hf * P : (hf + 1) * P, :])
+
+        def interleave(copy, c, a, b):
+            copy(
+                x_bf[c][:, a:b, :].rearrange("p (c i) t -> p c t i", i=4),
+                x_raw[c][:, :, a:b].rearrange("p t (c i) -> p c t i", i=4),
+            )
+
+        for c in range(n_chunks):
+            if c < n_chunks - 1:
+                interleave(nc.vector.tensor_copy, c, 0, X_CHUNK)
+            else:
+                interleave(nc.vector.tensor_copy, c, 0, X_LAST_VECTOR)
+                interleave(nc.scalar.copy, c, X_LAST_VECTOR, X_CHUNK)
+            cols = slice(c * X_CHUNK, (c + 1) * X_CHUNK)
+            nc.vector.quantize_mx(
+                out=x_words[:, cols].bitcast(FP8X4),
+                scales=x_scales[:, cols],
+                in_=x_bf[c][:].rearrange("p w t -> p (w t)"),
+            )
+
+        def gather_tokens(e):
+            if e in GATHER_GROUPS:
+                a, b = GATHER_GROUPS[e]
+                lst = offs_sb[:, a * C // 16 : b * C // 16]
+                nc.vector.tensor_copy(g_words[:, a * C : b * C], x_words[:].indirect(lst))
+                nc.vector.tensor_copy(g_scales[:, a * C : b * C], x_scales[:].indirect(lst))
+
+        def first_layer(e, bank, w, s):
+            g = [i for i, (a, b) in enumerate(W_GROUPS) if a <= e < b][0]
+            nc.tensor.matmul_mx(
+                out=bank[e % 2][:],
+                lhsT=g_words[:, e * C : (e + 1) * C].bitcast(FP8X4),
+                lhsT_scale=g_scales[:, e * C : (e + 1) * C],
+                rhs=w[g][:, e - W_GROUPS[g][0], :].bitcast(FP4X4),
+                rhs_scale=s,
+                start=True,
+                stop=True,
+            )
+
+        def by_word(ap):
+            return ap.rearrange("s (m u d) -> s u m d", u=2, d=2)
+
+        def in_order(ap):
+            return ap.rearrange("s (u m d) -> s u m d", u=2, d=2)
+
+        def relu(e):
+            nc.scalar.activation(in_order(relu_a[e][:]), by_word(bank_a[e % 2][:]), RELU)
+
+        def product(e):
+            nc.vector.tensor_tensor(in_order(h_rows[e][:]), by_word(bank_b[e % 2][:]), in_order(relu_a[e][:]), MULT)
+
+        def turn(e):
+            words = h_rows[e][:].bitcast(F32)
+            for u in range(2):
+                nc.tensor.transpose(bank_t[e % 2][:, u * P : (u + 1) * P], words[:, u * P : (u + 1) * P], ident[:])
+            nc.scalar.copy(
+                h_cols[e][:].bitcast(F32).rearrange("p (s u) -> p s u", u=2),
+                bank_t[e % 2][:, : 2 * P].rearrange("p (u s) -> p s u", u=2),
+            )
+
+        def quantise_h(e):
+            nc.vector.quantize_mx(out=h_words[e][:].bitcast(FP8X4), scales=h_scales[e][:], in_=h_cols[e][:])
+
+        def second_layer(e, hf, dst):
+            nc.tensor.matmul_mx(
+                out=dst,
+                lhsT=w2[e // 4][:, e % 4, hf * 2 * P : (hf + 1) * 2 * P].bitcast(FP4X4),
+                lhsT_scale=s2[:, e, hf * P : (hf + 1) * P],
+                rhs=h_words[e][:].bitcast(FP8X4),
+                rhs_scale=h_scales[e][:],
+                start=True,
+                stop=True,
+            )
+
+        def finish(e):
+            g = [i for i, (a, b) in enumerate(Y_GROUPS) if a <= e < b][0]
+            a, b = Y_GROUPS[g]
+            quantise_h(e)
+            second_layer(e, 0, bank_y[g % 2][:, (e - a) * C : (e - a + 1) * C])
+            if e == b - 1:
+                nc.scalar.copy(y[0][:, a * C : b * C], bank_y[g % 2][:, : (b - a) * C])
+
+        for e in range(2):
+            gather_tokens(e)
+            first_layer(e, bank_a, w1, s1[e // 4][:, e % 4, :])
+            first_layer(e, bank_b, w3, s3[:, e, :])
+        for e in range(E):
+            relu(e)
+            gather_tokens(e + 2)
+            if e + 2 < E:
+                first_layer(e + 2, bank_a, w1, s1[(e + 2) // 4][:, (e + 2) % 4, :])
+            product(e)
+            turn(e)
+            if e + 2 < E:
+                first_layer(e + 2, bank_b, w3, s3[:, e + 2, :])
+            if e > 0:
+                finish(e - 1)
+        finish(E - 1)
+        for g in range(2):
+            for e in range(4 * g, 4 * g + 4):
+                second_layer(e, 1, bank_a[g][:, (e % 4) * C : (e % 4 + 1) * C])
+            nc.scalar.copy(y[1][:, g * 4 * C : (g + 1) * 4 * C], bank_a[g][:])
+
+        def fetch(hf, r, a, b):
+            nc.vector.tensor_tensor(
+                prod[hf][r][:, a:b], y[hf][:].indirect(pos_sb[r][:, a // 16 : b // 16]), gate_sb[hf][r][:, a:b], MULT
+            )
+
+        pieces = [(0, 512), (512, T)]
+        sum_banks = [bank_b, bank_y]
+        back_banks = [bank_t, bank_a]
+        for hf in range(2):
+            on_pe = [3, 2, 1, 0] if hf == 0 else [3, 2, 1]
+            for r in on_pe:
+                fetch(hf, r, 0, T)
+                for i, (a, b) in enumerate(pieces):
+                    for c in range(a, b, P):
+                        nc.tensor.matmul(
+                            sum_banks[hf][i][:, c - a : c - a + P],
+                            prod[hf][r][:, c : c + P],
+                            ident[:],
+                            start=(r == on_pe[0] and c == a),
+                            stop=(r == on_pe[-1] and c == b - P),
+                            is_transpose=True,
+                        )
+            if hf == 1:
+                fetch(hf, 0, 0, T)
+            for i, (a, b) in enumerate(pieces):
+                nc.scalar.copy(turned[hf][:, a:b], sum_banks[hf][i][:, : b - a])
+            for i, (a, b) in enumerate(pieces):
+                for c in range(a, b, P):
+                    nc.tensor.transpose(back_banks[hf][i][:, c - a : c - a + P], turned[hf][:, c : c + P], ident[:])
+                if hf == 0:
+                    nc.scalar.copy(res[hf][:, a:b], back_banks[hf][i][:, : b - a])
+                else:
+                    nc.vector.tensor_tensor(res[hf][:, a:b], back_banks[hf][i][:, : b - a], prod[hf][0][:, a:b], ADD)
+                nc.sync.dma_start(out=out[hf * P : (hf + 1) * P, a:b], in_=res[hf][:, a:b])

@@ -24,8 +24,8 @@ P = 128
 X_CHUNK = 256
 X_LAST_VECTOR = 160
 W_GROUPS = [(0, 1), (1, 2), (2, 4), (4, 6), (6, 8)]
-GATHER_GROUPS = {0: (0, 1), 1: (1, 2), 2: (2, 4), 4: (4, 6), 6: (6, 8)}
-Y_GROUPS = [(0, 2), (2, 4), (4, 6), (6, 7), (7, 8)]
+GATHER_GROUPS = [(0, 1), (1, 3), (3, 5), (5, 8)]
+DEPTH = 3
 
 
 def tile_moe_ecr_glu_relu_kernel(
@@ -48,7 +48,7 @@ def tile_moe_ecr_glu_relu_kernel(
         x_scales = sb("x_scales", [P, T], U8)
         g_words = sb("g_words", [P, S], U32)
         g_scales = sb("g_scales", [P, S], U8)
-        s1 = [sb("s1_%d" % h, [P, 4, H], U8) for h in range(2)]
+        s1 = sb("s1", [P, E, H], U8)
         s3 = sb("s3", [P, E, H], U8)
         s2 = sb("s2", [P, E, N], U8)
         w1 = [sb("w1_%d" % a, [P, b - a, 2 * H], U8) for a, b in W_GROUPS]
@@ -67,10 +67,9 @@ def tile_moe_ecr_glu_relu_kernel(
         turned = [sb("turned%d" % hf, [P, T], F32) for hf in range(2)]
         res = [sb("res%d" % hf, [P, T], F32) for hf in range(2)]
 
-        bank_a = [psum.tile([P, 512], F32, name="bank_a%d" % i) for i in range(2)]
-        bank_b = [psum.tile([P, 512], F32, name="bank_b%d" % i) for i in range(2)]
+        bank_a = [psum.tile([P, 512], F32, name="bank_a%d" % i) for i in range(DEPTH)]
+        bank_b = [psum.tile([P, 512], F32, name="bank_b%d" % i) for i in range(DEPTH)]
         bank_t = [psum.tile([P, 512], F32, name="bank_t%d" % i) for i in range(2)]
-        bank_y = [psum.tile([P, 512], F32, name="bank_y%d" % i) for i in range(2)]
 
         def zero(t):
             nc.vector.memset(t[:].rearrange("p e n -> p (e n)").bitcast(I32), 0)
@@ -85,9 +84,9 @@ def tile_moe_ecr_glu_relu_kernel(
         def load_words(dst, src, a, b):
             nc.sync.dma_start(out=dst[:].bitcast(I32), in_=src[a:b, 0].rearrange("e p n -> p e n").bitcast(I32))
 
+        make_identity(nc, ident[:])
+        zero(s1)
         zero(s3)
-        zero(s1[0])
-        zero(s1[1])
         zero(s2)
         nc.vector.memset(x_scales[:].bitcast(I32), 0)
         for hf in range(2):
@@ -101,21 +100,17 @@ def tile_moe_ecr_glu_relu_kernel(
                 out=x_raw[c][:], in_=xT[:, c * X_CHUNK : (c + 1) * X_CHUNK].rearrange("(p j) w -> p j w", j=4)
             )
         load_scales(nc.gpsimd, s3, w3_scales, 0, E)
-        load_scales(nc.sync, s1[0], w1_scales, 0, 4)
-        make_identity(nc, ident[:])
+        load_scales(nc.sync, s1, w1_scales, 0, E)
         for g in range(len(W_GROUPS)):
-            if g == 3:
-                load_scales(nc.sync, s1[1], w1_scales, 4, 8)
             load_words(w1[g], w1_words, *W_GROUPS[g])
             load_words(w3[g], w3_words, *W_GROUPS[g])
         load_scales(nc.sync, s2, w2_scales, 0, E)
         load_words(w2[0], w2_words, 0, 4)
         load_words(w2[1], w2_words, 4, 8)
-        for r, pos in enumerate((pos1, pos2, pos3, pos4)):
-            nc.sync.dma_start(pos_sb[r][:], pos)
-        for hf in range(2):
-            for r in reversed(range(TOP)):
-                nc.sync.dma_start(out=gate_sb[hf][r][:], in_=gate[r, hf * P : (hf + 1) * P, :])
+        for hf, r in [(hf, r) for hf in range(2) for r in (3, 2, 1)] + [(0, 0), (1, 0)]:
+            nc.sync.dma_start(out=gate_sb[hf][r][:], in_=gate[r, hf * P : (hf + 1) * P, :])
+            if hf == 0:
+                nc.sync.dma_start(pos_sb[r][:], (pos1, pos2, pos3, pos4)[r])
 
         def interleave(copy, c, a, b):
             copy(
@@ -124,7 +119,9 @@ def tile_moe_ecr_glu_relu_kernel(
             )
 
         for c in range(n_chunks):
-            if c < n_chunks - 1:
+            if c == 0:
+                interleave(nc.scalar.copy, c, 0, X_CHUNK)
+            elif c < n_chunks - 1:
                 interleave(nc.vector.tensor_copy, c, 0, X_CHUNK)
             else:
                 interleave(nc.vector.tensor_copy, c, 0, X_LAST_VECTOR)
@@ -136,17 +133,15 @@ def tile_moe_ecr_glu_relu_kernel(
                 in_=x_bf[c][:].rearrange("p w t -> p (w t)"),
             )
 
-        def gather_tokens(e):
-            if e in GATHER_GROUPS:
-                a, b = GATHER_GROUPS[e]
-                lst = offs_sb[:, a * C // 16 : b * C // 16]
-                nc.vector.tensor_copy(g_words[:, a * C : b * C], x_words[:].indirect(lst))
-                nc.vector.tensor_copy(g_scales[:, a * C : b * C], x_scales[:].indirect(lst))
+        def gather_tokens(a, b):
+            lst = offs_sb[:, a * C // 16 : b * C // 16]
+            nc.vector.tensor_copy(g_words[:, a * C : b * C], x_words[:].indirect(lst))
+            nc.vector.tensor_copy(g_scales[:, a * C : b * C], x_scales[:].indirect(lst))
 
         def first_layer(e, bank, w, s):
             g = [i for i, (a, b) in enumerate(W_GROUPS) if a <= e < b][0]
             nc.tensor.matmul_mx(
-                out=bank[e % 2][:],
+                out=bank[e % DEPTH][:],
                 lhsT=g_words[:, e * C : (e + 1) * C].bitcast(FP8X4),
                 lhsT_scale=g_scales[:, e * C : (e + 1) * C],
                 rhs=w[g][:, e - W_GROUPS[g][0], :].bitcast(FP4X4),
@@ -162,10 +157,10 @@ def tile_moe_ecr_glu_relu_kernel(
             return ap.rearrange("s (u m d) -> s u m d", u=2, d=2)
 
         def relu(e):
-            nc.scalar.activation(in_order(relu_a[e][:]), by_word(bank_a[e % 2][:]), RELU)
+            nc.scalar.activation(in_order(relu_a[e][:]), by_word(bank_a[e % DEPTH][:]), RELU)
 
         def product(e):
-            nc.vector.tensor_tensor(in_order(h_rows[e][:]), by_word(bank_b[e % 2][:]), in_order(relu_a[e][:]), MULT)
+            nc.vector.tensor_tensor(in_order(h_rows[e][:]), by_word(bank_b[e % DEPTH][:]), in_order(relu_a[e][:]), MULT)
 
         def turn(e):
             words = h_rows[e][:].bitcast(F32)
@@ -190,34 +185,37 @@ def tile_moe_ecr_glu_relu_kernel(
                 stop=True,
             )
 
-        def finish(e):
-            g = [i for i, (a, b) in enumerate(Y_GROUPS) if a <= e < b][0]
-            a, b = Y_GROUPS[g]
-            quantise_h(e)
-            second_layer(e, 0, bank_y[g % 2][:, (e - a) * C : (e - a + 1) * C])
-            if e == b - 1:
-                nc.scalar.copy(y[0][:, a * C : b * C], bank_y[g % 2][:, : (b - a) * C])
+        def up(e):
+            first_layer(e, bank_a, w1, s1[:, e, :])
 
-        for e in range(2):
-            gather_tokens(e)
-            first_layer(e, bank_a, w1, s1[e // 4][:, e % 4, :])
+        def up3(e):
             first_layer(e, bank_b, w3, s3[:, e, :])
+
+        for a, b in GATHER_GROUPS:
+            gather_tokens(a, b)
+        for e in range(DEPTH):
+            up(e)
+            up3(e)
         for e in range(E):
             relu(e)
-            gather_tokens(e + 2)
-            if e + 2 < E:
-                first_layer(e + 2, bank_a, w1, s1[(e + 2) // 4][:, (e + 2) % 4, :])
+            if e + DEPTH < E:
+                up(e + DEPTH)
             product(e)
             turn(e)
-            if e + 2 < E:
-                first_layer(e + 2, bank_b, w3, s3[:, e + 2, :])
-            if e > 0:
-                finish(e - 1)
-        finish(E - 1)
-        for g in range(2):
-            for e in range(4 * g, 4 * g + 4):
-                second_layer(e, 1, bank_a[g][:, (e % 4) * C : (e % 4 + 1) * C])
-            nc.scalar.copy(y[1][:, g * 4 * C : (g + 1) * 4 * C], bank_a[g][:])
+            if e + DEPTH < E:
+                up3(e + DEPTH)
+        for hf, groups in enumerate(
+            (
+                ((bank_a[2], 0, 4), (bank_b[2], 4, 7), (bank_a[0], 7, 8)),
+                ((bank_b[0], 0, 4), (bank_a[1], 4, 8)),
+            )
+        ):
+            for bank, a, b in groups:
+                for e in range(a, b):
+                    if hf == 0:
+                        quantise_h(e)
+                    second_layer(e, hf, bank[:, (e - a) * C : (e - a + 1) * C])
+                nc.scalar.copy(y[hf][:, a * C : b * C], bank[:, : (b - a) * C])
 
         def fetch(hf, r, a, b):
             nc.vector.tensor_tensor(
@@ -225,10 +223,10 @@ def tile_moe_ecr_glu_relu_kernel(
             )
 
         pieces = [(0, 512), (512, T)]
-        sum_banks = [bank_b, bank_y]
-        back_banks = [bank_t, bank_a]
+        sum_banks = [bank_t, (bank_a[2], bank_b[2])]
+        back_banks = [(bank_b[1], bank_a[0]), (bank_b[0], bank_a[1])]
+        on_pe = [3, 2, 1]
         for hf in range(2):
-            on_pe = [3, 2, 1, 0] if hf == 0 else [3, 2, 1]
             for r in on_pe:
                 fetch(hf, r, 0, T)
                 for i, (a, b) in enumerate(pieces):
@@ -241,15 +239,21 @@ def tile_moe_ecr_glu_relu_kernel(
                             stop=(r == on_pe[-1] and c == b - P),
                             is_transpose=True,
                         )
-            if hf == 1:
-                fetch(hf, 0, 0, T)
             for i, (a, b) in enumerate(pieces):
                 nc.scalar.copy(turned[hf][:, a:b], sum_banks[hf][i][:, : b - a])
             for i, (a, b) in enumerate(pieces):
                 for c in range(a, b, P):
                     nc.tensor.transpose(back_banks[hf][i][:, c - a : c - a + P], turned[hf][:, c : c + P], ident[:])
-                if hf == 0:
-                    nc.scalar.copy(res[hf][:, a:b], back_banks[hf][i][:, : b - a])
-                else:
-                    nc.vector.tensor_tensor(res[hf][:, a:b], back_banks[hf][i][:, : b - a], prod[hf][0][:, a:b], ADD)
-                nc.sync.dma_start(out=out[hf * P : (hf + 1) * P, a:b], in_=res[hf][:, a:b])
+
+        def finish(hf, i):
+            a, b = pieces[i]
+            nc.vector.tensor_tensor(res[hf][:, a:b], back_banks[hf][i][:, : b - a], prod[hf][0][:, a:b], ADD)
+            nc.sync.dma_start(out=out[hf * P : (hf + 1) * P, a:b], in_=res[hf][:, a:b])
+
+        fetch(0, 0, 0, T)
+        fetch(1, 0, *pieces[0])
+        finish(0, 0)
+        finish(0, 1)
+        fetch(1, 0, *pieces[1])
+        finish(1, 0)
+        finish(1, 1)

@@ -23,9 +23,10 @@ RELU = mybir.ActivationFunctionType.Relu
 P = 128
 X_CHUNK = 256
 X_LAST_VECTOR = 160
-W_GROUPS = [(0, 1), (1, 2), (2, 4), (4, 6), (6, 8)]
-GATHER_GROUPS = [(0, 1), (1, 3), (3, 5), (5, 8)]
-DEPTH = 3
+W1_GROUPS = [(0, 2), (2, 5), (5, 8)]
+W3_GROUPS = [(0, 4), (4, 8)]
+GATHER_GROUPS = [(0, 1), (1, 3), (3, 5), (5, 7), (7, 8)]
+TURN_GROUPS = [(0, 2), (2, 4), (4, 6), (6, 7), (7, 8)]
 
 
 def tile_moe_ecr_glu_relu_kernel(
@@ -36,8 +37,8 @@ def tile_moe_ecr_glu_relu_kernel(
         keep = ctx.enter_context(tc.tile_pool(name="keep", bufs=1))
         psum = ctx.enter_context(tc.psum_pool(name="psum", bufs=1))
 
-        def sb(name, shape, dtype):
-            return keep.tile(shape, dtype, name=name, align_bytes=64)
+        def sb(name, shape, dtype, tag=None):
+            return keep.tile(shape, dtype, name=name, tag=tag or name, align_bytes=64)
 
         offs_sb = sb("offs_sb", [P, S // 16], U16)
         pos_sb = [sb("pos_sb%d" % r, [P, T // 16], U16) for r in range(TOP)]
@@ -51,28 +52,27 @@ def tile_moe_ecr_glu_relu_kernel(
         s1 = sb("s1", [P, E, H], U8)
         s3 = sb("s3", [P, E, H], U8)
         s2 = sb("s2", [P, E, N], U8)
-        w1 = [sb("w1_%d" % a, [P, b - a, 2 * H], U8) for a, b in W_GROUPS]
-        w3 = [sb("w3_%d" % a, [P, b - a, 2 * H], U8) for a, b in W_GROUPS]
+        w1 = [sb("w1_%d" % a, [P, b - a, 2 * H], U8) for a, b in W1_GROUPS]
+        w3 = [sb("w3_%d" % a, [P, b - a, 2 * H], U8) for a, b in W3_GROUPS]
         w2 = [sb("w2_%d" % h, [P, 4, 2 * N], U8) for h in range(2)]
-        gate_sb = [[sb("gate%d_%d" % (hf, r), [P, T], F32) for r in range(TOP)] for hf in range(2)]
+        gate_sb = [sb("gate%d" % r, [P, T], F32) for r in range(TOP)]
         ident = sb("ident", [P, P], F32)
         warm = sb("warm", [P, 8], F32)
         relu_a = [sb("relu_a%d" % e, [P, H], F32) for e in range(E)]
         h_rows = [sb("h_rows%d" % e, [P, H], BF16) for e in range(E)]
-        h_cols = [sb("h_cols%d" % e, [P, H], BF16) for e in range(E)]
-        h_words = [sb("h_words%d" % e, [P, C], U32) for e in range(E)]
-        h_scales = [sb("h_scales%d" % e, [P, C], U8) for e in range(E)]
+        h_cols = [sb("h_cols%d" % a, [P, (b - a) * H], BF16) for a, b in TURN_GROUPS]
+        h_scales = [sb("h_scales%d" % a, [P, (b - a) * C], U8) for a, b in TURN_GROUPS]
         y = [sb("y%d" % hf, [P, S + PAD], F32) for hf in range(2)]
         prod = [[sb("prod%d_%d" % (hf, r), [P, T], F32) for r in range(TOP)] for hf in range(2)]
         turned = [sb("turned%d" % hf, [P, T], F32) for hf in range(2)]
         res = [sb("res%d" % hf, [P, T], F32) for hf in range(2)]
 
-        bank_a = [psum.tile([P, 512], F32, name="bank_a%d" % i) for i in range(DEPTH)]
-        bank_b = [psum.tile([P, 512], F32, name="bank_b%d" % i) for i in range(DEPTH)]
-        bank_t = [psum.tile([P, 512], F32, name="bank_t%d" % i) for i in range(2)]
+        banks = [psum.tile([P, 512], F32, name="bank%d" % i) for i in range(8)]
+        bank_a, bank_b = [banks[0], banks[1], banks[6], banks[7]], banks[2:6]
+        bank_t = [bank_a[2], bank_a[3]]
 
-        def zero(t):
-            nc.vector.memset(t[:].rearrange("p e n -> p (e n)").bitcast(I32), 0)
+        def zero(eng, t):
+            eng.memset(t[:].rearrange("p e n -> p (e n)").bitcast(I32), 0)
 
         def load_scales(eng, plane, src, a, b):
             for r in range(4):
@@ -84,10 +84,10 @@ def tile_moe_ecr_glu_relu_kernel(
         def load_words(dst, src, a, b):
             nc.sync.dma_start(out=dst[:].bitcast(I32), in_=src[a:b, 0].rearrange("e p n -> p e n").bitcast(I32))
 
+        zero(nc.vector, s1)
+        zero(nc.gpsimd, s3)
         make_identity(nc, ident[:])
-        zero(s1)
-        zero(s3)
-        zero(s2)
+        zero(nc.vector, s2)
         nc.vector.memset(x_scales[:].bitcast(I32), 0)
         for hf in range(2):
             nc.vector.memset(y[hf][:, S:], 0.0)
@@ -99,18 +99,19 @@ def tile_moe_ecr_glu_relu_kernel(
             nc.sync.dma_start(
                 out=x_raw[c][:], in_=xT[:, c * X_CHUNK : (c + 1) * X_CHUNK].rearrange("(p j) w -> p j w", j=4)
             )
-        load_scales(nc.gpsimd, s3, w3_scales, 0, E)
+        load_words(w1[0], w1_words, *W1_GROUPS[0])
         load_scales(nc.sync, s1, w1_scales, 0, E)
-        for g in range(len(W_GROUPS)):
-            load_words(w1[g], w1_words, *W_GROUPS[g])
-            load_words(w3[g], w3_words, *W_GROUPS[g])
+        load_words(w1[1], w1_words, *W1_GROUPS[1])
+        load_scales(nc.sync, s3, w3_scales, 0, E)
+        load_words(w3[0], w3_words, *W3_GROUPS[0])
+        load_words(w1[2], w1_words, *W1_GROUPS[2])
+        load_words(w3[1], w3_words, *W3_GROUPS[1])
         load_scales(nc.sync, s2, w2_scales, 0, E)
         load_words(w2[0], w2_words, 0, 4)
         load_words(w2[1], w2_words, 4, 8)
-        for hf, r in [(hf, r) for hf in range(2) for r in (3, 2, 1)] + [(0, 0), (1, 0)]:
-            nc.sync.dma_start(out=gate_sb[hf][r][:], in_=gate[r, hf * P : (hf + 1) * P, :])
-            if hf == 0:
-                nc.sync.dma_start(pos_sb[r][:], (pos1, pos2, pos3, pos4)[r])
+        for r in (3, 2, 1, 0):
+            nc.sync.dma_start(out=gate_sb[r][:], in_=gate[r, 0:P, :])
+            nc.sync.dma_start(pos_sb[r][:], (pos1, pos2, pos3, pos4)[r])
 
         def interleave(copy, c, a, b):
             copy(
@@ -138,17 +139,28 @@ def tile_moe_ecr_glu_relu_kernel(
             nc.vector.tensor_copy(g_words[:, a * C : b * C], x_words[:].indirect(lst))
             nc.vector.tensor_copy(g_scales[:, a * C : b * C], x_scales[:].indirect(lst))
 
-        def first_layer(e, bank, w, s):
-            g = [i for i, (a, b) in enumerate(W_GROUPS) if a <= e < b][0]
+        def group_of(groups, e):
+            return [i for i, (a, b) in enumerate(groups) if a <= e < b][0]
+
+        def first_layer(e, bank, w, s, groups):
+            g = group_of(groups, e)
+            cols = slice(e * C, (e + 1) * C)
             nc.tensor.matmul_mx(
-                out=bank[e % DEPTH][:],
-                lhsT=g_words[:, e * C : (e + 1) * C].bitcast(FP8X4),
-                lhsT_scale=g_scales[:, e * C : (e + 1) * C],
-                rhs=w[g][:, e - W_GROUPS[g][0], :].bitcast(FP4X4),
-                rhs_scale=s,
+                out=bank[:],
+                lhsT=g_words[:, cols].bitcast(FP8X4),
+                lhsT_scale=g_scales[:, cols],
+                rhs=w[g][:, e - groups[g][0], :].bitcast(FP4X4),
+                rhs_scale=s[:, e, :],
                 start=True,
                 stop=True,
             )
+
+        def up_a(e):
+            first_layer(e, bank_a[e % 4], w1, s1, W1_GROUPS)
+            relu(e)
+
+        def up_b(e):
+            first_layer(e, bank_b[e % 4], w3, s3, W3_GROUPS)
 
         def by_word(ap):
             return ap.rearrange("s (m u d) -> s u m d", u=2, d=2)
@@ -157,103 +169,128 @@ def tile_moe_ecr_glu_relu_kernel(
             return ap.rearrange("s (u m d) -> s u m d", u=2, d=2)
 
         def relu(e):
-            nc.scalar.activation(in_order(relu_a[e][:]), by_word(bank_a[e % DEPTH][:]), RELU)
+            nc.scalar.activation(in_order(relu_a[e][:]), by_word(bank_a[e % 4][:]), RELU)
 
         def product(e):
-            nc.vector.tensor_tensor(in_order(h_rows[e][:]), by_word(bank_b[e % DEPTH][:]), in_order(relu_a[e][:]), MULT)
+            nc.vector.tensor_tensor(in_order(h_rows[e][:]), by_word(bank_b[e % 4][:]), in_order(relu_a[e][:]), MULT)
 
-        def turn(e):
-            words = h_rows[e][:].bitcast(F32)
-            for u in range(2):
-                nc.tensor.transpose(bank_t[e % 2][:, u * P : (u + 1) * P], words[:, u * P : (u + 1) * P], ident[:])
+        def turn(g):
+            a, b = TURN_GROUPS[g]
+            bank = bank_t[g % 2]
+            for e in range(a, b):
+                words = h_rows[e][:].bitcast(F32)
+                for u in range(2):
+                    c = (2 * (e - a) + u) * P
+                    nc.tensor.transpose(bank[:, c : c + P], words[:, u * P : (u + 1) * P], ident[:])
             nc.scalar.copy(
-                h_cols[e][:].bitcast(F32).rearrange("p (s u) -> p s u", u=2),
-                bank_t[e % 2][:, : 2 * P].rearrange("p (u s) -> p s u", u=2),
+                h_cols[g][:].bitcast(F32).rearrange("p (e s u) -> p e s u", u=2, s=C),
+                bank[:, : (b - a) * 2 * P].rearrange("p (e u s) -> p e s u", u=2, s=C),
             )
 
-        def quantise_h(e):
-            nc.vector.quantize_mx(out=h_words[e][:].bitcast(FP8X4), scales=h_scales[e][:], in_=h_cols[e][:])
+        h_words = {}
 
-        def second_layer(e, hf, dst):
-            nc.tensor.matmul_mx(
-                out=dst,
-                lhsT=w2[e // 4][:, e % 4, hf * 2 * P : (hf + 1) * 2 * P].bitcast(FP4X4),
-                lhsT_scale=s2[:, e, hf * P : (hf + 1) * P],
-                rhs=h_words[e][:].bitcast(FP8X4),
-                rhs_scale=h_scales[e][:],
-                start=True,
-                stop=True,
-            )
+        def quantise_h(g, tag=None):
+            a, b = TURN_GROUPS[g]
+            h_words.setdefault(g, sb("h_words%d" % a, [P, (b - a) * C], U32, tag))
+            nc.vector.quantize_mx(out=h_words[g][:].bitcast(FP8X4), scales=h_scales[g][:], in_=h_cols[g][:])
 
-        def up(e):
-            first_layer(e, bank_a, w1, s1[:, e, :])
-
-        def up3(e):
-            first_layer(e, bank_b, w3, s3[:, e, :])
+        def second_layer(hf, a, b, bank, copy=nc.scalar.copy):
+            for e in range(a, b):
+                g = group_of(TURN_GROUPS, e)
+                cols = slice((e - TURN_GROUPS[g][0]) * C, (e - TURN_GROUPS[g][0] + 1) * C)
+                nc.tensor.matmul_mx(
+                    out=bank[:, (e - a) * C : (e - a + 1) * C],
+                    lhsT=w2[e // 4][:, e % 4, hf * 2 * P : (hf + 1) * 2 * P].bitcast(FP4X4),
+                    lhsT_scale=s2[:, e, hf * P : (hf + 1) * P],
+                    rhs=h_words[g][:, cols].bitcast(FP8X4),
+                    rhs_scale=h_scales[g][:, cols],
+                    start=True,
+                    stop=True,
+                )
+            copy(y[hf][:, a * C : b * C], bank[:, : (b - a) * C])
 
         for a, b in GATHER_GROUPS:
             gather_tokens(a, b)
-        for e in range(DEPTH):
-            up(e)
-            up3(e)
-        for e in range(E):
-            relu(e)
-            if e + DEPTH < E:
-                up(e + DEPTH)
-            product(e)
-            turn(e)
-            if e + DEPTH < E:
-                up3(e + DEPTH)
-        for hf, groups in enumerate(
-            (
-                ((bank_a[2], 0, 4), (bank_b[2], 4, 7), (bank_a[0], 7, 8)),
-                ((bank_b[0], 0, 4), (bank_a[1], 4, 8)),
-            )
-        ):
-            for bank, a, b in groups:
-                for e in range(a, b):
-                    if hf == 0:
-                        quantise_h(e)
-                    second_layer(e, hf, bank[:, (e - a) * C : (e - a + 1) * C])
-                nc.scalar.copy(y[hf][:, a * C : b * C], bank[:, : (b - a) * C])
+        for e in range(5):
+            up_a(e)
+        for e in range(4):
+            up_b(e)
+        for e in range(5, E):
+            up_a(e)
+        product(0)
+        product(1)
+        up_b(4)
+        up_b(5)
+        turn(0)
+        product(2)
+        product(3)
+        up_b(6)
+        up_b(7)
+        turn(1)
+        product(4)
+        product(5)
+        turn(2)
+        product(6)
+        turn(3)
+        product(7)
+        turn(4)
+        quantise_h(0, "relu_a7")
+        second_layer(0, 0, 2, bank_a[1])
+        quantise_h(1, "relu_a6")
+        second_layer(0, 2, 4, bank_b[0])
+        quantise_h(2)
+        second_layer(0, 4, 6, bank_b[1])
+        quantise_h(3)
+        quantise_h(4)
+        second_layer(0, 6, 8, bank_a[0], nc.vector.tensor_copy)
+        second_layer(1, 0, 4, banks[0])
+        second_layer(1, 4, 8, banks[0])
 
         def fetch(hf, r, a, b):
             nc.vector.tensor_tensor(
-                prod[hf][r][:, a:b], y[hf][:].indirect(pos_sb[r][:, a // 16 : b // 16]), gate_sb[hf][r][:, a:b], MULT
+                prod[hf][r][:, a:b], y[hf][:].indirect(pos_sb[r][:, a // 16 : b // 16]), gate_sb[r][:, a:b], MULT
             )
 
-        pieces = [(0, 512), (512, T)]
-        sum_banks = [bank_t, (bank_a[2], bank_b[2])]
-        back_banks = [(bank_b[1], bank_a[0]), (bank_b[0], bank_a[1])]
-        on_pe = [3, 2, 1]
-        for hf in range(2):
-            for r in on_pe:
-                fetch(hf, r, 0, T)
-                for i, (a, b) in enumerate(pieces):
-                    for c in range(a, b, P):
-                        nc.tensor.matmul(
-                            sum_banks[hf][i][:, c - a : c - a + P],
-                            prod[hf][r][:, c : c + P],
-                            ident[:],
-                            start=(r == on_pe[0] and c == a),
-                            stop=(r == on_pe[-1] and c == b - P),
-                            is_transpose=True,
-                        )
-            for i, (a, b) in enumerate(pieces):
-                nc.scalar.copy(turned[hf][:, a:b], sum_banks[hf][i][:, : b - a])
-            for i, (a, b) in enumerate(pieces):
-                for c in range(a, b, P):
-                    nc.tensor.transpose(back_banks[hf][i][:, c - a : c - a + P], turned[hf][:, c : c + P], ident[:])
+        def add_turned(hf, r, a, b, bank, first, last):
+            for c in range(a, b, P):
+                nc.tensor.matmul(
+                    bank[:, c - a : c - a + P],
+                    prod[hf][r][:, c : c + P],
+                    ident[:],
+                    start=(first and c == a),
+                    stop=(last and c == b - P),
+                    is_transpose=True,
+                )
 
-        def finish(hf, i):
-            a, b = pieces[i]
-            nc.vector.tensor_tensor(res[hf][:, a:b], back_banks[hf][i][:, : b - a], prod[hf][0][:, a:b], ADD)
+        def turn_back(hf, a, b, sum_bank, back_bank):
+            nc.scalar.copy(turned[hf][:, a:b], sum_bank[:, : b - a])
+            for c in range(a, b, P):
+                nc.tensor.transpose(back_bank[:, c - a : c - a + P], turned[hf][:, c : c + P], ident[:])
+
+        def store(hf, a, b):
             nc.sync.dma_start(out=out[hf * P : (hf + 1) * P, a:b], in_=res[hf][:, a:b])
 
-        fetch(0, 0, 0, T)
-        fetch(1, 0, *pieces[0])
-        finish(0, 0)
-        finish(0, 1)
-        fetch(1, 0, *pieces[1])
-        finish(1, 0)
-        finish(1, 1)
+        pieces0 = [(0, 512, banks[4], banks[1]), (512, T, banks[5], banks[7])]
+        for r in (3, 2, 1, 0):
+            fetch(0, r, 0, T)
+            for a, b, sum_bank, back_bank in pieces0:
+                add_turned(0, r, a, b, sum_bank, r == 3, r == 0)
+        for a, b, sum_bank, back_bank in pieces0:
+            turn_back(0, a, b, sum_bank, back_bank)
+        for a, b, sum_bank, back_bank in pieces0:
+            nc.scalar.copy(res[0][:, a:b], back_bank[:, : b - a])
+            store(0, a, b)
+
+        pieces1 = [(0, 256, banks[2], banks[0]), (256, 512, banks[3], banks[4]), (512, T, banks[6], banks[5])]
+        for r in (3, 2):
+            fetch(1, r, 0, T)
+            for a, b, sum_bank, back_bank in pieces1:
+                add_turned(1, r, a, b, sum_bank, r == 3, False)
+        for a, b, sum_bank, back_bank in pieces1:
+            fetch(1, 1, a, b)
+            add_turned(1, 1, a, b, sum_bank, False, True)
+            turn_back(1, a, b, sum_bank, back_bank)
+        fetch(1, 0, 0, T)
+        for a, b, sum_bank, back_bank in pieces1:
+            nc.vector.tensor_tensor(res[1][:, a:b], back_bank[:, : b - a], prod[1][0][:, a:b], ADD)
+            store(1, a, b)

@@ -262,35 +262,32 @@ def tile_moe_ecr_glu_relu_kernel(
                     is_transpose=True,
                 )
 
-        def turn_back(hf, a, b, sum_bank, back_bank):
-            nc.scalar.copy(turned[hf][:, a:b], sum_bank[:, : b - a])
-            for c in range(a, b, P):
-                nc.tensor.transpose(back_bank[:, c - a : c - a + P], turned[hf][:, c : c + P], ident[:])
-
         def store(hf, a, b):
             nc.sync.dma_start(out=out[hf * P : (hf + 1) * P, a:b], in_=res[hf][:, a:b])
 
-        pieces0 = [(0, 512, banks[4], banks[1]), (512, T, banks[5], banks[7])]
-        for r in (3, 2, 1, 0):
-            fetch(0, r, 0, T)
-            for a, b, sum_bank, back_bank in pieces0:
-                add_turned(0, r, a, b, sum_bank, r == 3, r == 0)
-        for a, b, sum_bank, back_bank in pieces0:
-            turn_back(0, a, b, sum_bank, back_bank)
-        for a, b, sum_bank, back_bank in pieces0:
-            nc.scalar.copy(res[0][:, a:b], back_bank[:, : b - a])
-            store(0, a, b)
+        pieces = [(0, 512), (512, T)]
+        sum_banks = [(banks[4], banks[5]), (banks[2], banks[3])]
+        back_banks = [(banks[1], banks[7]), (banks[6], banks[0])]
+        for hf in range(2):
+            for r in (3, 2, 1):
+                fetch(hf, r, 0, T)
+                for i, (a, b) in enumerate(pieces):
+                    add_turned(hf, r, a, b, sum_banks[hf][i], r == 3, r == 1)
+            for i, (a, b) in enumerate(pieces):
+                nc.scalar.copy(turned[hf][:, a:b], sum_banks[hf][i][:, : b - a])
+            for i, (a, b) in enumerate(pieces):
+                for c in range(a, b, P):
+                    nc.tensor.transpose(back_banks[hf][i][:, c - a : c - a + P], turned[hf][:, c : c + P], ident[:])
 
-        pieces1 = [(0, 256, banks[2], banks[0]), (256, 512, banks[3], banks[4]), (512, T, banks[6], banks[5])]
-        for r in (3, 2):
-            fetch(1, r, 0, T)
-            for a, b, sum_bank, back_bank in pieces1:
-                add_turned(1, r, a, b, sum_bank, r == 3, False)
-        for a, b, sum_bank, back_bank in pieces1:
-            fetch(1, 1, a, b)
-            add_turned(1, 1, a, b, sum_bank, False, True)
-            turn_back(1, a, b, sum_bank, back_bank)
-        fetch(1, 0, 0, T)
-        for a, b, sum_bank, back_bank in pieces1:
-            nc.vector.tensor_tensor(res[1][:, a:b], back_bank[:, : b - a], prod[1][0][:, a:b], ADD)
-            store(1, a, b)
+        def finish(hf, i):
+            a, b = pieces[i]
+            nc.vector.tensor_tensor(res[hf][:, a:b], back_banks[hf][i][:, : b - a], prod[hf][0][:, a:b], ADD)
+            store(hf, a, b)
+
+        fetch(0, 0, 0, T)
+        fetch(1, 0, *pieces[0])
+        finish(0, 0)
+        finish(0, 1)
+        fetch(1, 0, *pieces[1])
+        finish(1, 0)
+        finish(1, 1)

@@ -21,11 +21,12 @@ ADD = mybir.AluOpType.add
 RELU = mybir.ActivationFunctionType.Relu
 
 P = 128
-X_CHUNK = 256
-X_LAST_VECTOR = 160
-W1_GROUPS = [(0, 2), (2, 5), (5, 8)]
-W3_GROUPS = [(0, 4), (4, 8)]
-GATHER_GROUPS = [(0, 1), (1, 3), (3, 5), (5, 7), (7, 8)]
+X_LOADS = [(0, 256), (256, 512), (512, 640), (640, 768)]
+X_CASTS = [(0, 0, 256, "vector"), (1, 256, 424, "vector"), (1, 424, 512, "scalar"), (2, 512, 640, "scalar"), (3, 640, 768, "vector")]
+X_QUANT = 256
+W1_GROUPS = [(0, 2), (2, 4), (4, 6), (6, 8)]
+W3_GROUPS = W1_GROUPS
+GATHER_GROUPS = [(0, 1), (1, 3), (3, 6), (6, 8)]
 TURN_GROUPS = [(0, 2), (2, 4), (4, 6), (6, 7), (7, 8)]
 
 
@@ -42,9 +43,8 @@ def tile_moe_ecr_glu_relu_kernel(
 
         offs_sb = sb("offs_sb", [P, S // 16], U16)
         pos_sb = [sb("pos_sb%d" % r, [P, T // 16], U16) for r in range(TOP)]
-        n_chunks = T // X_CHUNK
-        x_raw = [sb("x_raw%d" % c, [P, 4, X_CHUNK], F32) for c in range(n_chunks)]
-        x_bf = [sb("x_bf%d" % c, [P, X_CHUNK, 4], BF16) for c in range(n_chunks)]
+        x_raw = [sb("x_raw%d" % a, [P, 4, b - a], F32) for a, b in X_LOADS]
+        x_bf = [sb("x_bf%d" % c, [P, X_QUANT, 4], BF16) for c in range(T // X_QUANT)]
         x_words = sb("x_words", [P, T], U32)
         x_scales = sb("x_scales", [P, T], U8)
         g_words = sb("g_words", [P, S], U32)
@@ -68,8 +68,9 @@ def tile_moe_ecr_glu_relu_kernel(
         res = [sb("res%d" % hf, [P, T], F32) for hf in range(2)]
 
         banks = [psum.tile([P, 512], F32, name="bank%d" % i) for i in range(8)]
-        bank_a, bank_b = [banks[0], banks[1], banks[6], banks[7]], banks[2:6]
-        bank_t = [bank_a[2], bank_a[3]]
+        bank_a = [banks[i] for i in (0, 1, 6, 7, 0, 1, 2, 3)]
+        bank_b = [banks[i] for i in (2, 3, 4, 5, 6, 7, 4, 5)]
+        bank_t = [banks[i] for i in (2, 3, 0, 1, 2)]
 
         def zero(eng, t):
             eng.memset(t[:].rearrange("p e n -> p (e n)").bitcast(I32), 0)
@@ -94,44 +95,39 @@ def tile_moe_ecr_glu_relu_kernel(
         nc.vector.memset(warm[:, 0:4], 0.0)
         nc.scalar.activation(warm[:, 4:8], warm[:, 0:4], RELU)
 
+        for c, (a, b) in enumerate(X_LOADS):
+            nc.sync.dma_start(out=x_raw[c][:], in_=xT[:, a:b].rearrange("(p j) w -> p j w", j=4))
         nc.sync.dma_start(offs_sb[:], offs)
-        for c in range(n_chunks):
-            nc.sync.dma_start(
-                out=x_raw[c][:], in_=xT[:, c * X_CHUNK : (c + 1) * X_CHUNK].rearrange("(p j) w -> p j w", j=4)
-            )
-        load_words(w1[0], w1_words, *W1_GROUPS[0])
         load_scales(nc.sync, s1, w1_scales, 0, E)
+        load_words(w1[0], w1_words, *W1_GROUPS[0])
         load_words(w1[1], w1_words, *W1_GROUPS[1])
         load_scales(nc.sync, s3, w3_scales, 0, E)
-        load_words(w3[0], w3_words, *W3_GROUPS[0])
-        load_words(w1[2], w1_words, *W1_GROUPS[2])
-        load_words(w3[1], w3_words, *W3_GROUPS[1])
-        load_scales(nc.sync, s2, w2_scales, 0, E)
+        for w, src, g in ((w3, w3_words, 0), (w1, w1_words, 2), (w3, w3_words, 1), (w3, w3_words, 2), (w1, w1_words, 3), (w3, w3_words, 3)):
+            load_words(w[g], src, *W1_GROUPS[g])
         load_words(w2[0], w2_words, 0, 4)
         load_words(w2[1], w2_words, 4, 8)
+        load_scales(nc.sync, s2, w2_scales, 0, E)
         for r in (3, 2, 1, 0):
             nc.sync.dma_start(out=gate_sb[r][:], in_=gate[r, 0:P, :])
             nc.sync.dma_start(pos_sb[r][:], (pos1, pos2, pos3, pos4)[r])
 
-        def interleave(copy, c, a, b):
+        def interleave(c, a, b, engine):
+            copy = nc.vector.tensor_copy if engine == "vector" else nc.scalar.copy
+            q, first = a // X_QUANT, X_LOADS[c][0]
             copy(
-                x_bf[c][:, a:b, :].rearrange("p (c i) t -> p c t i", i=4),
-                x_raw[c][:, :, a:b].rearrange("p t (c i) -> p c t i", i=4),
+                x_bf[q][:, a - q * X_QUANT : b - q * X_QUANT, :].rearrange("p (c i) t -> p c t i", i=4),
+                x_raw[c][:, :, a - first : b - first].rearrange("p t (c i) -> p c t i", i=4),
             )
 
-        for c in range(n_chunks):
-            if c == 0:
-                interleave(nc.scalar.copy, c, 0, X_CHUNK)
-            elif c < n_chunks - 1:
-                interleave(nc.vector.tensor_copy, c, 0, X_CHUNK)
-            else:
-                interleave(nc.vector.tensor_copy, c, 0, X_LAST_VECTOR)
-                interleave(nc.scalar.copy, c, X_LAST_VECTOR, X_CHUNK)
-            cols = slice(c * X_CHUNK, (c + 1) * X_CHUNK)
+        for q in range(T // X_QUANT):
+            for cast in X_CASTS:
+                if cast[1] // X_QUANT == q:
+                    interleave(*cast)
+            cols = slice(q * X_QUANT, (q + 1) * X_QUANT)
             nc.vector.quantize_mx(
                 out=x_words[:, cols].bitcast(FP8X4),
                 scales=x_scales[:, cols],
-                in_=x_bf[c][:].rearrange("p w t -> p (w t)"),
+                in_=x_bf[q][:].rearrange("p w t -> p (w t)"),
             )
 
         def gather_tokens(a, b):
@@ -156,11 +152,11 @@ def tile_moe_ecr_glu_relu_kernel(
             )
 
         def up_a(e):
-            first_layer(e, bank_a[e % 4], w1, s1, W1_GROUPS)
+            first_layer(e, bank_a[e], w1, s1, W1_GROUPS)
             relu(e)
 
         def up_b(e):
-            first_layer(e, bank_b[e % 4], w3, s3, W3_GROUPS)
+            first_layer(e, bank_b[e], w3, s3, W3_GROUPS)
 
         def by_word(ap):
             return ap.rearrange("s (m u d) -> s u m d", u=2, d=2)
@@ -169,14 +165,14 @@ def tile_moe_ecr_glu_relu_kernel(
             return ap.rearrange("s (u m d) -> s u m d", u=2, d=2)
 
         def relu(e):
-            nc.scalar.activation(in_order(relu_a[e][:]), by_word(bank_a[e % 4][:]), RELU)
+            nc.scalar.activation(in_order(relu_a[e][:]), by_word(bank_a[e][:]), RELU)
 
         def product(e):
-            nc.vector.tensor_tensor(in_order(h_rows[e][:]), by_word(bank_b[e % 4][:]), in_order(relu_a[e][:]), MULT)
+            nc.vector.tensor_tensor(in_order(h_rows[e][:]), by_word(bank_b[e][:]), in_order(relu_a[e][:]), MULT)
 
         def turn(g):
             a, b = TURN_GROUPS[g]
-            bank = bank_t[g % 2]
+            bank = bank_t[g]
             for e in range(a, b):
                 words = h_rows[e][:].bitcast(F32)
                 for u in range(2):
@@ -187,12 +183,13 @@ def tile_moe_ecr_glu_relu_kernel(
                 bank[:, : (b - a) * 2 * P].rearrange("p (e u s) -> p e s u", u=2, s=C),
             )
 
-        h_words = {}
-
-        def quantise_h(g, tag=None):
+        def quantise_h(g):
             a, b = TURN_GROUPS[g]
-            h_words.setdefault(g, sb("h_words%d" % a, [P, (b - a) * C], U32, tag))
-            nc.vector.quantize_mx(out=h_words[g][:].bitcast(FP8X4), scales=h_scales[g][:], in_=h_cols[g][:])
+            nc.vector.quantize_mx(
+                out=h_words[a // 4][:, (a % 4) * C : (a % 4 + b - a) * C].bitcast(FP8X4),
+                scales=h_scales[g][:],
+                in_=h_cols[g][:],
+            )
 
         def second_layer(hf, a, b, bank, copy=nc.scalar.copy):
             for e in range(a, b):
@@ -202,7 +199,7 @@ def tile_moe_ecr_glu_relu_kernel(
                     out=bank[:, (e - a) * C : (e - a + 1) * C],
                     lhsT=w2[e // 4][:, e % 4, hf * 2 * P : (hf + 1) * 2 * P].bitcast(FP4X4),
                     lhsT_scale=s2[:, e, hf * P : (hf + 1) * P],
-                    rhs=h_words[g][:, cols].bitcast(FP8X4),
+                    rhs=h_words[e // 4][:, (e % 4) * C : (e % 4 + 1) * C].bitcast(FP8X4),
                     rhs_scale=h_scales[g][:, cols],
                     start=True,
                     stop=True,
@@ -211,20 +208,22 @@ def tile_moe_ecr_glu_relu_kernel(
 
         for a, b in GATHER_GROUPS:
             gather_tokens(a, b)
-        for e in range(5):
-            up_a(e)
         for e in range(4):
-            up_b(e)
-        for e in range(5, E):
             up_a(e)
+        up_b(0)
+        up_b(1)
+        up_a(4)
+        up_a(5)
+        for e in range(2, 6):
+            up_b(e)
         product(0)
+        up_a(6)
         product(1)
-        up_b(4)
-        up_b(5)
+        up_a(7)
         turn(0)
         product(2)
-        product(3)
         up_b(6)
+        product(3)
         up_b(7)
         turn(1)
         product(4)
@@ -234,17 +233,18 @@ def tile_moe_ecr_glu_relu_kernel(
         turn(3)
         product(7)
         turn(4)
-        quantise_h(0, "relu_a7")
-        second_layer(0, 0, 2, bank_a[1])
-        quantise_h(1, "relu_a6")
-        second_layer(0, 2, 4, bank_b[0])
+        h_words = [sb("h_words0", [P, 4 * C], U32, "relu_a7"), sb("h_words1", [P, 4 * C], U32)]
+        quantise_h(0)
+        second_layer(0, 0, 2, banks[6])
+        quantise_h(1)
+        second_layer(0, 2, 4, banks[7])
         quantise_h(2)
-        second_layer(0, 4, 6, bank_b[1])
+        second_layer(0, 4, 6, banks[3])
         quantise_h(3)
         quantise_h(4)
-        second_layer(0, 6, 8, bank_a[0], nc.vector.tensor_copy)
-        second_layer(1, 0, 4, banks[0])
-        second_layer(1, 4, 8, banks[0])
+        second_layer(0, 6, 8, banks[4])
+        second_layer(1, 0, 4, banks[3])
+        second_layer(1, 4, 8, banks[4])
 
         def fetch(hf, r, a, b):
             nc.vector.tensor_tensor(
@@ -266,8 +266,8 @@ def tile_moe_ecr_glu_relu_kernel(
             nc.sync.dma_start(out=out[hf * P : (hf + 1) * P, a:b], in_=res[hf][:, a:b])
 
         pieces = [(0, 512), (512, T)]
-        sum_banks = [(banks[4], banks[5]), (banks[2], banks[3])]
-        back_banks = [(banks[1], banks[7]), (banks[6], banks[0])]
+        sum_banks = [(banks[5], banks[6]), (banks[2], banks[1])]
+        back_banks = [(banks[7], banks[0]), (banks[3], banks[4])]
         for hf in range(2):
             for r in (3, 2, 1):
                 fetch(hf, r, 0, T)

@@ -26,7 +26,7 @@ X_CASTS = [(0, 0, 256, "vector"), (1, 256, 424, "vector"), (1, 424, 512, "scalar
 X_QUANT = 256
 W1_GROUPS = [(0, 2), (2, 4), (4, 6), (6, 8)]
 W3_GROUPS = W1_GROUPS
-GATHER_GROUPS = [(0, 1), (1, 3), (3, 6), (6, 8)]
+GATHER_GROUPS = [(0, 1), (1, 3), (3, 5), (5, 7), (7, 8)]
 TURN_GROUPS = [(0, 2), (2, 4), (4, 6), (6, 7), (7, 8)]
 
 
@@ -63,14 +63,14 @@ def tile_moe_ecr_glu_relu_kernel(
         h_cols = [sb("h_cols%d" % a, [P, (b - a) * H], BF16) for a, b in TURN_GROUPS]
         h_scales = [sb("h_scales%d" % a, [P, (b - a) * C], U8) for a, b in TURN_GROUPS]
         y = [sb("y%d" % hf, [P, S + PAD], F32) for hf in range(2)]
-        prod = [[sb("prod%d_%d" % (hf, r), [P, T], F32) for r in range(TOP)] for hf in range(2)]
+        prod = {(hf, r): sb("prod%d_%d" % (hf, r), [P, T], F32) for hf in range(2) for r in range(TOP)}
         turned = [sb("turned%d" % hf, [P, T], F32) for hf in range(2)]
         res = [sb("res%d" % hf, [P, T], F32) for hf in range(2)]
 
         banks = [psum.tile([P, 512], F32, name="bank%d" % i) for i in range(8)]
-        bank_a = [banks[i] for i in (0, 1, 6, 7, 0, 1, 2, 3)]
-        bank_b = [banks[i] for i in (2, 3, 4, 5, 6, 7, 4, 5)]
-        bank_t = [banks[i] for i in (2, 3, 0, 1, 2)]
+        bank_a = [banks[i] for i in (0, 1, 6, 7, 0, 1, 6, 7)]
+        bank_b = [banks[i] for i in (2, 3, 4, 5, 2, 3, 4, 5)]
+        bank_t = [banks[i] for i in (6, 7, 0, 1, 6)]
 
         def zero(eng, t):
             eng.memset(t[:].rearrange("p e n -> p (e n)").bitcast(I32), 0)
@@ -102,7 +102,7 @@ def tile_moe_ecr_glu_relu_kernel(
         load_words(w1[0], w1_words, *W1_GROUPS[0])
         load_words(w1[1], w1_words, *W1_GROUPS[1])
         load_scales(nc.sync, s3, w3_scales, 0, E)
-        for w, src, g in ((w3, w3_words, 0), (w1, w1_words, 2), (w3, w3_words, 1), (w3, w3_words, 2), (w1, w1_words, 3), (w3, w3_words, 3)):
+        for w, src, g in ((w3, w3_words, 0), (w1, w1_words, 2), (w3, w3_words, 1), (w1, w1_words, 3), (w3, w3_words, 2), (w3, w3_words, 3)):
             load_words(w[g], src, *W1_GROUPS[g])
         load_words(w2[0], w2_words, 0, 4)
         load_words(w2[1], w2_words, 4, 8)
@@ -119,16 +119,20 @@ def tile_moe_ecr_glu_relu_kernel(
                 x_raw[c][:, :, a - first : b - first].rearrange("p t (c i) -> p c t i", i=4),
             )
 
-        for q in range(T // X_QUANT):
-            for cast in X_CASTS:
-                if cast[1] // X_QUANT == q:
-                    interleave(*cast)
-            cols = slice(q * X_QUANT, (q + 1) * X_QUANT)
+        def quantise_x(a, b):
+            q = a // X_QUANT
             nc.vector.quantize_mx(
-                out=x_words[:, cols].bitcast(FP8X4),
-                scales=x_scales[:, cols],
-                in_=x_bf[q][:].rearrange("p w t -> p (w t)"),
+                out=x_words[:, a:b].bitcast(FP8X4),
+                scales=x_scales[:, a:b],
+                in_=x_bf[q][:, a - q * X_QUANT : b - q * X_QUANT, :].rearrange("p w t -> p (w t)"),
             )
+
+        for cast in X_CASTS:
+            interleave(*cast)
+            if cast[0] < 2 and cast[2] == X_LOADS[cast[0]][1]:
+                quantise_x(*X_LOADS[cast[0]])
+        for c in (2, 3):
+            quantise_x(*X_LOADS[c])
 
         def gather_tokens(a, b):
             lst = offs_sb[:, a * C // 16 : b * C // 16]
@@ -186,7 +190,7 @@ def tile_moe_ecr_glu_relu_kernel(
         def quantise_h(g):
             a, b = TURN_GROUPS[g]
             nc.vector.quantize_mx(
-                out=h_words[a // 4][:, (a % 4) * C : (a % 4 + b - a) * C].bitcast(FP8X4),
+                out=h_words[:, a * C : b * C].bitcast(FP8X4),
                 scales=h_scales[g][:],
                 in_=h_cols[g][:],
             )
@@ -199,7 +203,7 @@ def tile_moe_ecr_glu_relu_kernel(
                     out=bank[:, (e - a) * C : (e - a + 1) * C],
                     lhsT=w2[e // 4][:, e % 4, hf * 2 * P : (hf + 1) * 2 * P].bitcast(FP4X4),
                     lhsT_scale=s2[:, e, hf * P : (hf + 1) * P],
-                    rhs=h_words[e // 4][:, (e % 4) * C : (e % 4 + 1) * C].bitcast(FP8X4),
+                    rhs=h_words[:, e * C : (e + 1) * C].bitcast(FP8X4),
                     rhs_scale=h_scales[g][:, cols],
                     start=True,
                     stop=True,
@@ -210,22 +214,17 @@ def tile_moe_ecr_glu_relu_kernel(
             gather_tokens(a, b)
         for e in range(4):
             up_a(e)
-        up_b(0)
-        up_b(1)
-        up_a(4)
-        up_a(5)
-        for e in range(2, 6):
-            up_b(e)
-        product(0)
-        up_a(6)
-        product(1)
-        up_a(7)
-        turn(0)
-        product(2)
-        up_b(6)
-        product(3)
-        up_b(7)
-        turn(1)
+        for k in range(2):
+            up_b(2 * k)
+            up_b(2 * k + 1)
+            up_a(2 * k + 4)
+            up_a(2 * k + 5)
+        for k in range(2):
+            product(2 * k)
+            up_b(2 * k + 4)
+            product(2 * k + 1)
+            up_b(2 * k + 5)
+            turn(k)
         product(4)
         product(5)
         turn(2)
@@ -233,29 +232,29 @@ def tile_moe_ecr_glu_relu_kernel(
         turn(3)
         product(7)
         turn(4)
-        h_words = [sb("h_words0", [P, 4 * C], U32, "relu_a7"), sb("h_words1", [P, 4 * C], U32)]
+        h_words = sb("h_words", [P, S], U32, "relu_a7")
         quantise_h(0)
-        second_layer(0, 0, 2, banks[6])
+        second_layer(0, 0, 2, banks[0])
         quantise_h(1)
-        second_layer(0, 2, 4, banks[7])
+        second_layer(0, 2, 4, banks[1])
         quantise_h(2)
-        second_layer(0, 4, 6, banks[3])
+        second_layer(0, 4, 6, banks[7], nc.vector.tensor_copy)
         quantise_h(3)
         quantise_h(4)
-        second_layer(0, 6, 8, banks[4])
-        second_layer(1, 0, 4, banks[3])
-        second_layer(1, 4, 8, banks[4])
+        second_layer(0, 6, 8, banks[2])
+        second_layer(1, 4, 8, banks[7])
+        second_layer(1, 0, 4, banks[2])
 
         def fetch(hf, r, a, b):
             nc.vector.tensor_tensor(
-                prod[hf][r][:, a:b], y[hf][:].indirect(pos_sb[r][:, a // 16 : b // 16]), gate_sb[r][:, a:b], MULT
+                prod[hf, r][:, a:b], y[hf][:].indirect(pos_sb[r][:, a // 16 : b // 16]), gate_sb[r][:, a:b], MULT
             )
 
         def add_turned(hf, r, a, b, bank, first, last):
             for c in range(a, b, P):
                 nc.tensor.matmul(
                     bank[:, c - a : c - a + P],
-                    prod[hf][r][:, c : c + P],
+                    prod[hf, r][:, c : c + P],
                     ident[:],
                     start=(first and c == a),
                     stop=(last and c == b - P),
@@ -266,8 +265,8 @@ def tile_moe_ecr_glu_relu_kernel(
             nc.sync.dma_start(out=out[hf * P : (hf + 1) * P, a:b], in_=res[hf][:, a:b])
 
         pieces = [(0, 512), (512, T)]
-        sum_banks = [(banks[5], banks[6]), (banks[2], banks[1])]
-        back_banks = [(banks[7], banks[0]), (banks[3], banks[4])]
+        sum_banks = [(banks[5], banks[4]), (banks[1], banks[6])]
+        back_banks = [(banks[3], banks[0]), (banks[2], banks[7])]
         for hf in range(2):
             for r in (3, 2, 1):
                 fetch(hf, r, 0, T)
@@ -281,7 +280,7 @@ def tile_moe_ecr_glu_relu_kernel(
 
         def finish(hf, i):
             a, b = pieces[i]
-            nc.vector.tensor_tensor(res[hf][:, a:b], back_banks[hf][i][:, : b - a], prod[hf][0][:, a:b], ADD)
+            nc.vector.tensor_tensor(res[hf][:, a:b], back_banks[hf][i][:, : b - a], prod[hf, 0][:, a:b], ADD)
             store(hf, a, b)
 
         fetch(0, 0, 0, T)

@@ -63,7 +63,8 @@ def tile_moe_ecr_glu_relu_kernel(
         h_cols = [sb("h_cols%d" % a, [P, (b - a) * H], BF16) for a, b in TURN_GROUPS]
         h_scales = [sb("h_scales%d" % a, [P, (b - a) * C], U8) for a, b in TURN_GROUPS]
         y = [sb("y%d" % hf, [P, S + PAD], F32) for hf in range(2)]
-        prod = {(hf, r): sb("prod%d_%d" % (hf, r), [P, T], F32) for hf in range(2) for r in range(TOP)}
+        prod = {(hf, r): sb("prod%d_%d" % (hf, r), [P, T], F32) for hf in range(2) for r in range(1, TOP)}
+        last = {(0, 0): sb("last0_0", [P, 512], F32), (0, 1): sb("last0_1", [P, 256], F32), (1, 0): sb("last1_0", [P, 512], F32)}
         turned = [sb("turned%d" % hf, [P, T], F32) for hf in range(2)]
         res = [sb("res%d" % hf, [P, T], F32) for hf in range(2)]
 
@@ -105,8 +106,8 @@ def tile_moe_ecr_glu_relu_kernel(
         for w, src, g in ((w3, w3_words, 0), (w1, w1_words, 2), (w3, w3_words, 1), (w1, w1_words, 3), (w3, w3_words, 2), (w3, w3_words, 3)):
             load_words(w[g], src, *W1_GROUPS[g])
         load_words(w2[0], w2_words, 0, 4)
-        load_words(w2[1], w2_words, 4, 8)
         load_scales(nc.sync, s2, w2_scales, 0, E)
+        load_words(w2[1], w2_words, 4, 8)
         for r in (3, 2, 1, 0):
             nc.sync.dma_start(out=gate_sb[r][:], in_=gate[r, 0:P, :])
             nc.sync.dma_start(pos_sb[r][:], (pos1, pos2, pos3, pos4)[r])
@@ -247,7 +248,7 @@ def tile_moe_ecr_glu_relu_kernel(
 
         def fetch(hf, r, a, b):
             nc.vector.tensor_tensor(
-                prod[hf, r][:, a:b], y[hf][:].indirect(pos_sb[r][:, a // 16 : b // 16]), gate_sb[r][:, a:b], MULT
+                prod[hf, r][:, a:b] if r else last[hf, a // 512][:], y[hf][:].indirect(pos_sb[r][:, a // 16 : b // 16]), gate_sb[r][:, a:b], MULT
             )
 
         def add_turned(hf, r, a, b, bank, first, last):
@@ -278,15 +279,18 @@ def tile_moe_ecr_glu_relu_kernel(
                 for c in range(a, b, P):
                     nc.tensor.transpose(back_banks[hf][i][:, c - a : c - a + P], turned[hf][:, c : c + P], ident[:])
 
-        def finish(hf, i):
-            a, b = pieces[i]
-            nc.vector.tensor_tensor(res[hf][:, a:b], back_banks[hf][i][:, : b - a], prod[hf, 0][:, a:b], ADD)
+        def finish(hf, a, b):
+            i = a // 512
+            first = pieces[i][0]
+            nc.vector.tensor_tensor(res[hf][:, a:b], back_banks[hf][i][:, a - first : b - first], last[hf, i][:, a - first : b - first], ADD)
             store(hf, a, b)
 
-        fetch(0, 0, 0, T)
+        fetch(0, 0, *pieces[0])
+        fetch(0, 0, *pieces[1])
         fetch(1, 0, *pieces[0])
-        finish(0, 0)
-        finish(0, 1)
+        finish(0, *pieces[0])
+        finish(0, *pieces[1])
+        last.setdefault((1, 1), sb("last1_1", [P, 256], F32, "last0_0"))
         fetch(1, 0, *pieces[1])
-        finish(1, 0)
-        finish(1, 1)
+        for a in range(0, T, 256):
+            finish(1, a, a + 256)

@@ -63,8 +63,7 @@ def tile_moe_ecr_glu_relu_kernel(
         h_cols = [sb("h_cols%d" % a, [P, (b - a) * H], BF16) for a, b in TURN_GROUPS]
         h_scales = [sb("h_scales%d" % a, [P, (b - a) * C], U8) for a, b in TURN_GROUPS]
         y = [sb("y%d" % hf, [P, S + PAD], F32) for hf in range(2)]
-        prod = {(hf, r): sb("prod%d_%d" % (hf, r), [P, T], F32) for hf in range(2) for r in range(1, TOP)}
-        last = {(0, 0): sb("last0_0", [P, 512], F32), (0, 1): sb("last0_1", [P, 256], F32), (1, 0): sb("last1_0", [P, 512], F32)}
+        prod = {(0, r): sb("prod0_%d" % r, [P, T], F32)[:] for r in range(TOP)}
         turned = [sb("turned%d" % hf, [P, T], F32) for hf in range(2)]
         res = [sb("res%d" % hf, [P, T], F32) for hf in range(2)]
 
@@ -247,9 +246,7 @@ def tile_moe_ecr_glu_relu_kernel(
         second_layer(1, 0, 4, banks[2])
 
         def fetch(hf, r, a, b):
-            nc.vector.tensor_tensor(
-                prod[hf, r][:, a:b] if r else last[hf, a // 512][:], y[hf][:].indirect(pos_sb[r][:, a // 16 : b // 16]), gate_sb[r][:, a:b], MULT
-            )
+            nc.vector.tensor_tensor(prod[hf, r][:, a:b], y[hf][:].indirect(pos_sb[r][:, a // 16 : b // 16]), gate_sb[r][:, a:b], MULT)
 
         def add_turned(hf, r, a, b, bank, first, last):
             for c in range(a, b, P):
@@ -262,35 +259,39 @@ def tile_moe_ecr_glu_relu_kernel(
                     is_transpose=True,
                 )
 
+        def turn_back(hf, a, b, sum_bank, back_bank):
+            nc.scalar.copy(turned[hf][:, a:b], sum_bank[:, : b - a])
+            for c in range(a, b, P):
+                nc.tensor.transpose(back_bank[:, c - a : c - a + P], turned[hf][:, c : c + P], ident[:])
+
         def store(hf, a, b):
             nc.sync.dma_start(out=out[hf * P : (hf + 1) * P, a:b], in_=res[hf][:, a:b])
 
-        pieces = [(0, 512), (512, T)]
-        sum_banks = [(banks[5], banks[4]), (banks[1], banks[6])]
-        back_banks = [(banks[3], banks[0]), (banks[2], banks[7])]
-        for hf in range(2):
-            for r in (3, 2, 1):
-                fetch(hf, r, 0, T)
-                for i, (a, b) in enumerate(pieces):
-                    add_turned(hf, r, a, b, sum_banks[hf][i], r == 3, r == 1)
-            for i, (a, b) in enumerate(pieces):
-                nc.scalar.copy(turned[hf][:, a:b], sum_banks[hf][i][:, : b - a])
-            for i, (a, b) in enumerate(pieces):
-                for c in range(a, b, P):
-                    nc.tensor.transpose(back_banks[hf][i][:, c - a : c - a + P], turned[hf][:, c : c + P], ident[:])
+        pieces = [(0, 512, banks[5], banks[3]), (512, T, banks[4], banks[0])]
+        for r in (3, 2, 1, 0):
+            fetch(0, r, 0, T)
+            for a, b, sum_bank, back_bank in pieces:
+                add_turned(0, r, a, b, sum_bank, r == 3, r == 0)
+        for a, b, sum_bank, back_bank in pieces:
+            turn_back(0, a, b, sum_bank, back_bank)
+        for a, b, sum_bank, back_bank in pieces:
+            nc.scalar.copy(res[0][:, a:b], back_bank[:, : b - a])
+            store(0, a, b)
 
-        def finish(hf, a, b):
-            i = a // 512
-            first = pieces[i][0]
-            nc.vector.tensor_tensor(res[hf][:, a:b], back_banks[hf][i][:, a - first : b - first], last[hf, i][:, a - first : b - first], ADD)
-            store(hf, a, b)
-
-        fetch(0, 0, *pieces[0])
-        fetch(0, 0, *pieces[1])
-        fetch(1, 0, *pieces[0])
-        finish(0, *pieces[0])
-        finish(0, *pieces[1])
-        last.setdefault((1, 1), sb("last1_1", [P, 256], F32, "last0_0"))
-        fetch(1, 0, *pieces[1])
-        for a in range(0, T, 256):
-            finish(1, a, a + 256)
+        later = sb("later", [P, TOP * T], F32, "prod0_1")
+        for r in range(TOP):
+            prod.setdefault((1, r), later[:, r * T : (r + 1) * T])
+        pieces = [(0, 256, banks[1], banks[7]), (256, 512, banks[6], banks[5]), (512, T, banks[2], banks[4])]
+        for r in (3, 2):
+            fetch(1, r, 0, T)
+            for a, b, sum_bank, back_bank in pieces:
+                add_turned(1, r, a, b, sum_bank, r == 3, False)
+        for a, b, sum_bank, back_bank in pieces:
+            fetch(1, 1, a, b)
+            add_turned(1, 1, a, b, sum_bank, False, True)
+            turn_back(1, a, b, sum_bank, back_bank)
+        fetch(1, 0, 0, 512)
+        fetch(1, 0, 512, T)
+        for a, b, sum_bank, back_bank in pieces:
+            nc.vector.tensor_tensor(res[1][:, a:b], back_bank[:, : b - a], prod[1, 0][:, a:b], ADD)
+            store(1, a, b)

@@ -55,7 +55,7 @@ def tile_moe_ecr_glu_relu_kernel(
         w1 = [sb("w1_%d" % a, [P, b - a, 2 * H], U8) for a, b in W1_GROUPS]
         w3 = [sb("w3_%d" % a, [P, b - a, 2 * H], U8) for a, b in W3_GROUPS]
         w2 = [sb("w2_%d" % h, [P, 4, 2 * N], U8) for h in range(2)]
-        gate_sb = [sb("gate%d" % r, [P, T], F32) for r in range(TOP)]
+        gate_sb = sb("gate_sb", [P, TOP, T], F32)
         ident = sb("ident", [P, P], F32)
         warm = sb("warm", [P, 8], F32)
         relu_a = [sb("relu_a%d" % e, [P, H], F32) for e in range(E)]
@@ -63,7 +63,7 @@ def tile_moe_ecr_glu_relu_kernel(
         h_cols = [sb("h_cols%d" % a, [P, (b - a) * H], BF16) for a, b in TURN_GROUPS]
         h_scales = [sb("h_scales%d" % a, [P, (b - a) * C], U8) for a, b in TURN_GROUPS]
         y = [sb("y%d" % hf, [P, S + PAD], F32) for hf in range(2)]
-        prod = {(0, r): sb("prod0_%d" % r, [P, T], F32)[:] for r in range(TOP)}
+        first_prod = [sb("first_prod%d" % r, [P, 512], F32) for r in range(TOP)]
         turned = [sb("turned%d" % hf, [P, T], F32) for hf in range(2)]
         res = [sb("res%d" % hf, [P, T], F32) for hf in range(2)]
 
@@ -107,9 +107,11 @@ def tile_moe_ecr_glu_relu_kernel(
         load_words(w2[0], w2_words, 0, 4)
         load_scales(nc.sync, s2, w2_scales, 0, E)
         load_words(w2[1], w2_words, 4, 8)
-        for r in (3, 2, 1, 0):
-            nc.sync.dma_start(out=gate_sb[r][:], in_=gate[r, 0:P, :])
-            nc.sync.dma_start(pos_sb[r][:], (pos1, pos2, pos3, pos4)[r])
+        for r0, r1 in ((0, 1), (1, 2), (2, 4)):
+            nc.sync.dma_start(out=gate_sb[:, r0:r1, 0:512], in_=gate[r0:r1, 0:P, 0:512].rearrange("r p w -> p r w"))
+            for r in range(r0, r1):
+                nc.sync.dma_start(pos_sb[r][:], (pos1, pos2, pos3, pos4)[r])
+        nc.sync.dma_start(out=gate_sb[:, :, 512:T], in_=gate[:, 0:P, 512:T].rearrange("r p w -> p r w"))
 
         def interleave(c, a, b, engine):
             copy = nc.vector.tensor_copy if engine == "vector" else nc.scalar.copy
@@ -245,17 +247,18 @@ def tile_moe_ecr_glu_relu_kernel(
         second_layer(1, 4, 8, banks[7])
         second_layer(1, 0, 4, banks[2])
 
-        def fetch(hf, r, a, b):
-            nc.vector.tensor_tensor(prod[hf, r][:, a:b], y[hf][:].indirect(pos_sb[r][:, a // 16 : b // 16]), gate_sb[r][:, a:b], MULT)
+        def fetch(dst, hf, r, a, b):
+            nc.vector.tensor_tensor(dst, y[hf][:].indirect(pos_sb[r][:, a // 16 : b // 16]), gate_sb[:, r, a:b], MULT)
 
-        def add_turned(hf, r, a, b, bank, first, last):
-            for c in range(a, b, P):
+        def add_turned(src, bank, first, last):
+            width = src.shape[1]
+            for c in range(0, width, P):
                 nc.tensor.matmul(
-                    bank[:, c - a : c - a + P],
-                    prod[hf, r][:, c : c + P],
+                    bank[:, c : c + P],
+                    src[:, c : c + P],
                     ident[:],
-                    start=(first and c == a),
-                    stop=(last and c == b - P),
+                    start=(first and c == 0),
+                    stop=(last and c == width - P),
                     is_transpose=True,
                 )
 
@@ -267,31 +270,31 @@ def tile_moe_ecr_glu_relu_kernel(
         def store(hf, a, b):
             nc.sync.dma_start(out=out[hf * P : (hf + 1) * P, a:b], in_=res[hf][:, a:b])
 
-        pieces = [(0, 512, banks[5], banks[3]), (512, T, banks[4], banks[0])]
-        for r in (3, 2, 1, 0):
-            fetch(0, r, 0, T)
-            for a, b, sum_bank, back_bank in pieces:
-                add_turned(0, r, a, b, sum_bank, r == 3, r == 0)
-        for a, b, sum_bank, back_bank in pieces:
+        def whole_sum(prods, a, b, sum_bank, back_bank):
+            for r in range(TOP):
+                fetch(prods[r], 0, r, a, b)
+                add_turned(prods[r], sum_bank, r == 0, r == TOP - 1)
             turn_back(0, a, b, sum_bank, back_bank)
-        for a, b, sum_bank, back_bank in pieces:
             nc.scalar.copy(res[0][:, a:b], back_bank[:, : b - a])
             store(0, a, b)
 
-        later = sb("later", [P, TOP * T], F32, "prod0_1")
-        for r in range(TOP):
-            prod.setdefault((1, r), later[:, r * T : (r + 1) * T])
+        whole_sum([t[:] for t in first_prod], 0, 512, banks[5], banks[3])
+        second = sb("second_prod", [P, TOP * 256], F32)
+        whole_sum([second[:, r * 256 : (r + 1) * 256] for r in range(TOP)], 512, T, banks[4], banks[0])
+
+        later = sb("later", [P, TOP * T], F32, "first_prod3")
+        prod = [later[:, r * T : (r + 1) * T] for r in range(TOP)]
         pieces = [(0, 256, banks[1], banks[7]), (256, 512, banks[6], banks[5]), (512, T, banks[2], banks[4])]
         for r in (3, 2):
-            fetch(1, r, 0, T)
+            fetch(prod[r], 1, r, 0, T)
             for a, b, sum_bank, back_bank in pieces:
-                add_turned(1, r, a, b, sum_bank, r == 3, False)
+                add_turned(prod[r][:, a:b], sum_bank, r == 3, False)
         for a, b, sum_bank, back_bank in pieces:
-            fetch(1, 1, a, b)
-            add_turned(1, 1, a, b, sum_bank, False, True)
+            fetch(prod[1][:, a:b], 1, 1, a, b)
+            add_turned(prod[1][:, a:b], sum_bank, False, True)
             turn_back(1, a, b, sum_bank, back_bank)
-        fetch(1, 0, 0, 512)
-        fetch(1, 0, 512, T)
+        fetch(prod[0][:, 0:512], 1, 0, 0, 512)
+        fetch(prod[0][:, 512:T], 1, 0, 512, T)
         for a, b, sum_bank, back_bank in pieces:
-            nc.vector.tensor_tensor(res[1][:, a:b], back_bank[:, : b - a], prod[1, 0][:, a:b], ADD)
+            nc.vector.tensor_tensor(res[1][:, a:b], back_bank[:, : b - a], prod[0][:, a:b], ADD)
             store(1, a, b)

@@ -19,6 +19,7 @@ FP4X4 = mybir.dt.float4_e2m1fn_x4
 MULT = mybir.AluOpType.mult
 ADD = mybir.AluOpType.add
 RELU = mybir.ActivationFunctionType.Relu
+COPY = mybir.ActivationFunctionType.Copy
 
 P = 128
 X_LOADS = [(0, 256), (256, 512), (512, 640), (640, 768)]
@@ -28,6 +29,8 @@ W1_GROUPS = [(0, 2), (2, 4), (4, 6), (6, 8)]
 W3_GROUPS = W1_GROUPS
 GATHER_GROUPS = [(0, 1), (1, 3), (3, 5), (5, 7), (7, 8)]
 TURN_GROUPS = [(0, 2), (2, 4), (4, 6), (6, 7), (7, 8)]
+TV = 384
+CHUNKS = (T - TV) // P
 
 
 def tile_moe_ecr_glu_relu_kernel(
@@ -55,7 +58,11 @@ def tile_moe_ecr_glu_relu_kernel(
         w1 = [sb("w1_%d" % a, [P, b - a, 2 * H], U8) for a, b in W1_GROUPS]
         w3 = [sb("w3_%d" % a, [P, b - a, 2 * H], U8) for a, b in W3_GROUPS]
         w2 = [sb("w2_%d" % h, [P, 4, 2 * N], U8) for h in range(2)]
-        gate_sb = sb("gate_sb", [P, TOP, T], F32)
+        gate_first = sb("gate_first", [P, T], F32)
+        gate_rest = [sb("gate_rest%d" % r, [P, TV], F32) for r in range(1, TOP)]
+        gate_rows = sb("gate_rows", [P, T - TV], F32)
+        gate_col1 = sb("gate_col1", [P, CHUNKS], F32)
+        gate_col23 = sb("gate_col23", [P, CHUNKS, 2], F32)
         ident = sb("ident", [P, P], F32)
         warm = sb("warm", [P, 8], F32)
         relu_a = [sb("relu_a%d" % e, [P, H], F32) for e in range(E)]
@@ -63,9 +70,8 @@ def tile_moe_ecr_glu_relu_kernel(
         h_cols = [sb("h_cols%d" % a, [P, (b - a) * H], BF16) for a, b in TURN_GROUPS]
         h_scales = [sb("h_scales%d" % a, [P, (b - a) * C], U8) for a, b in TURN_GROUPS]
         y = [sb("y%d" % hf, [P, S + PAD], F32) for hf in range(2)]
-        first_prod = [sb("first_prod%d" % r, [P, 512], F32) for r in range(TOP)]
-        turned = [sb("turned%d" % hf, [P, T], F32) for hf in range(2)]
-        res = [sb("res%d" % hf, [P, T], F32) for hf in range(2)]
+        turned = [sb("turned%d" % hf, [P, TV], F32) for hf in range(2)]
+        res = sb("res", [P, 2, T], F32)
 
         banks = [psum.tile([P, 512], F32, name="bank%d" % i) for i in range(8)]
         bank_a = [banks[i] for i in (0, 1, 6, 7, 0, 1, 6, 7)]
@@ -87,6 +93,8 @@ def tile_moe_ecr_glu_relu_kernel(
 
         zero(nc.vector, s1)
         zero(nc.gpsimd, s3)
+        nc.gpsimd.memset(gate_rows[:], 0.0)
+        nc.gpsimd.dma_start(out=gate_rows[0 : TOP - 1, :], in_=gate[1:TOP, 0, TV:T])
         make_identity(nc, ident[:])
         zero(nc.vector, s2)
         nc.vector.memset(x_scales[:].bitcast(I32), 0)
@@ -107,11 +115,18 @@ def tile_moe_ecr_glu_relu_kernel(
         load_words(w2[0], w2_words, 0, 4)
         load_scales(nc.sync, s2, w2_scales, 0, E)
         load_words(w2[1], w2_words, 4, 8)
-        for r0, r1 in ((0, 1), (1, 2), (2, 4)):
-            nc.sync.dma_start(out=gate_sb[:, r0:r1, 0:512], in_=gate[r0:r1, 0:P, 0:512].rearrange("r p w -> p r w"))
-            for r in range(r0, r1):
-                nc.sync.dma_start(pos_sb[r][:], (pos1, pos2, pos3, pos4)[r])
-        nc.sync.dma_start(out=gate_sb[:, :, 512:T], in_=gate[:, 0:P, 512:T].rearrange("r p w -> p r w"))
+        for r in (1, 2, 3, 0):
+            nc.sync.dma_start(pos_sb[r][:], (pos1, pos2, pos3, pos4)[r])
+            if r:
+                nc.sync.dma_start(out=gate_rest[r - 1][:], in_=gate[r, 0:P, 0:TV])
+            else:
+                nc.sync.dma_start(out=gate_first[:], in_=gate[0, 0:P, :])
+
+        for c in range(CHUNKS):
+            nc.tensor.transpose(banks[7][:, c * P : (c + 1) * P], gate_rows[:, c * P : (c + 1) * P], ident[:])
+        by_chunk = banks[7][:, : CHUNKS * P].rearrange("p (c r) -> p c r", r=P)
+        nc.scalar.copy(gate_col1[:], by_chunk[:, :, 0])
+        nc.scalar.copy(gate_col23[:], by_chunk[:, :, 1:3])
 
         def interleave(c, a, b, engine):
             copy = nc.vector.tensor_copy if engine == "vector" else nc.scalar.copy
@@ -247,54 +262,80 @@ def tile_moe_ecr_glu_relu_kernel(
         second_layer(1, 4, 8, banks[7])
         second_layer(1, 0, 4, banks[2])
 
-        def fetch(dst, hf, r, a, b):
-            nc.vector.tensor_tensor(dst, y[hf][:].indirect(pos_sb[r][:, a // 16 : b // 16]), gate_sb[:, r, a:b], MULT)
+        def offsets(r, a, b):
+            return pos_sb[r][:, a // 16 : b // 16]
 
-        def add_turned(src, bank, first, last):
-            width = src.shape[1]
-            for c in range(0, width, P):
-                nc.tensor.matmul(
-                    bank[:, c : c + P],
-                    src[:, c : c + P],
-                    ident[:],
-                    start=(first and c == 0),
-                    stop=(last and c == width - P),
-                    is_transpose=True,
-                )
+        def add_turned(dst, src, start, stop):
+            nc.tensor.matmul(dst, src, ident[:], start=start, stop=stop, is_transpose=True)
 
-        def turn_back(hf, a, b, sum_bank, back_bank):
-            nc.scalar.copy(turned[hf][:, a:b], sum_bank[:, : b - a])
-            for c in range(a, b, P):
-                nc.tensor.transpose(back_bank[:, c - a : c - a + P], turned[hf][:, c : c + P], ident[:])
+        def store(h0, h1, a, b):
+            nc.sync.dma_start(out=out[h0 * P : h1 * P, a:b].rearrange("(h p) t -> p h t", p=P), in_=res[:, h0:h1, a:b])
 
-        def store(hf, a, b):
-            nc.sync.dma_start(out=out[hf * P : (hf + 1) * P, a:b], in_=res[hf][:, a:b])
+        sum_banks = [banks[5], banks[4]]
+        plain_banks = {1: (banks[3], banks[6]), 2: (banks[0], banks[1]), 3: (banks[3], banks[6])}
+        back_banks = [banks[7], banks[2]]
+        groups = [(0, 2), (2, 3)]
+        first = sb("first", [P, 2, T], F32)
 
-        def whole_sum(prods, a, b, sum_bank, back_bank):
-            for r in range(TOP):
-                fetch(prods[r], 0, r, a, b)
-                add_turned(prods[r], sum_bank, r == 0, r == TOP - 1)
-            turn_back(0, a, b, sum_bank, back_bank)
-            nc.scalar.copy(res[0][:, a:b], back_bank[:, : b - a])
-            store(0, a, b)
+        def gated_sum(hf):
+            for r in range(1, TOP):
+                prod = sb("prod%d%d" % (hf, r), [P, TV], F32)
+                nc.vector.tensor_tensor(prod[:], y[hf][:].indirect(offsets(r, 0, TV)), gate_rest[r - 1][:], MULT)
+                for c in range(0, TV, P):
+                    add_turned(sum_banks[hf][:, c : c + P], prod[:, c : c + P], r == 1 and c == 0, r == TOP - 1 and c == TV - P)
 
-        whole_sum([t[:] for t in first_prod], 0, 512, banks[5], banks[3])
-        second = sb("second_prod", [P, TOP * 256], F32)
-        whole_sum([second[:, r * 256 : (r + 1) * 256] for r in range(TOP)], 512, T, banks[4], banks[0])
+        def gated_back(hf):
+            nc.scalar.copy(turned[hf][:], sum_banks[hf][:, :TV])
+            for c in range(0, TV, P):
+                nc.tensor.transpose(sum_banks[hf][:, c : c + P], turned[hf][:, c : c + P], ident[:])
 
-        later = sb("later", [P, TOP * T], F32, "first_prod3")
-        prod = [later[:, r * T : (r + 1) * T] for r in range(TOP)]
-        pieces = [(0, 256, banks[1], banks[7]), (256, 512, banks[6], banks[5]), (512, T, banks[2], banks[4])]
-        for r in (3, 2):
-            fetch(prod[r], 1, r, 0, T)
-            for a, b, sum_bank, back_bank in pieces:
-                add_turned(prod[r][:, a:b], sum_bank, r == 3, False)
-        for a, b, sum_bank, back_bank in pieces:
-            fetch(prod[1][:, a:b], 1, 1, a, b)
-            add_turned(prod[1][:, a:b], sum_bank, False, True)
-            turn_back(1, a, b, sum_bank, back_bank)
-        fetch(prod[0][:, 0:512], 1, 0, 0, 512)
-        fetch(prod[0][:, 512:T], 1, 0, 512, T)
-        for a, b, sum_bank, back_bank in pieces:
-            nc.vector.tensor_tensor(res[1][:, a:b], back_bank[:, : b - a], prod[0][:, a:b], ADD)
-            store(1, a, b)
+        def plain_fetch(r):
+            got = []
+            for hf in range(2):
+                t = sb("plain%d%d" % (hf, r), [P, T - TV], F32, "gate_col1" if (r, hf) == (3, 0) else None)
+                nc.scalar.activation(t[:], y[hf][:].indirect(offsets(r, TV, T)), COPY)
+                got.append(t)
+            for g, (c0, c1) in enumerate(groups):
+                for c in range(c0, c1):
+                    for hf in range(2):
+                        col = (2 * (c - c0) + hf) * P
+                        nc.tensor.transpose(plain_banks[r][g][:, col : col + P], got[hf][:, c * P : (c + 1) * P], ident[:])
+
+        def plain_back(r):
+            scaled = sb("scaled%d" % r, [P, CHUNKS, 2 * P], F32)
+            for g, (c0, c1) in enumerate(groups):
+                for c in range(c0, c1):
+                    col = 2 * (c - c0) * P
+                    factor = gate_col1[:, c : c + 1] if r == 1 else gate_col23[:, c, r - 2 : r - 1]
+                    nc.scalar.activation(scaled[:, c, :], plain_banks[r][g][:, col : col + 2 * P], COPY, scale=factor)
+                for c in range(c0, c1):
+                    for hf in range(2):
+                        col = (hf * (c1 - c0) + c - c0) * P
+                        add_turned(
+                            back_banks[g][:, col : col + P],
+                            scaled[:, c, hf * P : (hf + 1) * P],
+                            r == 1 and c == c0 and hf == 0,
+                            r == TOP - 1 and c == c1 - 1 and hf == 1,
+                        )
+
+        gated_sum(0)
+        plain_fetch(1)
+        gated_sum(1)
+        plain_fetch(2)
+        plain_back(1)
+        plain_fetch(3)
+        plain_back(2)
+        gated_back(0)
+        gated_back(1)
+        plain_back(3)
+        for hf in range(2):
+            nc.vector.tensor_tensor(first[:, hf, :], y[hf][:].indirect(offsets(0, 0, T)), gate_first[:], MULT)
+        for hf in range(2):
+            nc.vector.tensor_tensor(res[:, hf, :TV], sum_banks[hf][:, :TV], first[:, hf, :TV], ADD)
+            store(hf, hf + 1, 0, TV)
+        for g, (c0, c1) in enumerate(groups):
+            a, b = TV + c0 * P, TV + c1 * P
+            nc.vector.tensor_tensor(
+                res[:, :, a:b], back_banks[g][:, : 2 * (b - a)].rearrange("p (h t) -> p h t", h=2), first[:, :, a:b], ADD
+            )
+            store(0, 2, a, b)

@@ -29,7 +29,7 @@ W1_GROUPS = [(0, 2), (2, 4), (4, 6), (6, 8)]
 W3_GROUPS = W1_GROUPS
 GATHER_GROUPS = [(0, 1), (1, 3), (3, 5), (5, 7), (7, 8)]
 TURN_GROUPS = [(0, 2), (2, 4), (4, 6), (6, 7), (7, 8)]
-TV = 384
+TV = 512
 CHUNKS = (T - TV) // P
 
 
@@ -70,8 +70,6 @@ def tile_moe_ecr_glu_relu_kernel(
         h_cols = [sb("h_cols%d" % a, [P, (b - a) * H], BF16) for a, b in TURN_GROUPS]
         h_scales = [sb("h_scales%d" % a, [P, (b - a) * C], U8) for a, b in TURN_GROUPS]
         y = [sb("y%d" % hf, [P, S + PAD], F32) for hf in range(2)]
-        turned = [sb("turned%d" % hf, [P, TV], F32) for hf in range(2)]
-        res = sb("res", [P, 2, T], F32)
 
         banks = [psum.tile([P, 512], F32, name="bank%d" % i) for i in range(8)]
         bank_a = [banks[i] for i in (0, 1, 6, 7, 0, 1, 6, 7)]
@@ -93,9 +91,8 @@ def tile_moe_ecr_glu_relu_kernel(
 
         zero(nc.vector, s1)
         zero(nc.gpsimd, s3)
-        nc.gpsimd.memset(gate_rows[:], 0.0)
-        nc.gpsimd.dma_start(out=gate_rows[0 : TOP - 1, :], in_=gate[1:TOP, 0, TV:T])
         make_identity(nc, ident[:])
+        nc.gpsimd.memset(gate_rows[:], 0.0)
         zero(nc.vector, s2)
         nc.vector.memset(x_scales[:].bitcast(I32), 0)
         for hf in range(2):
@@ -114,19 +111,14 @@ def tile_moe_ecr_glu_relu_kernel(
             load_words(w[g], src, *W1_GROUPS[g])
         load_words(w2[0], w2_words, 0, 4)
         load_scales(nc.sync, s2, w2_scales, 0, E)
-        load_words(w2[1], w2_words, 4, 8)
+        nc.sync.dma_start(out=gate_rows[0 : TOP - 1, :], in_=gate[1:TOP, 0, TV:T])
         for r in (1, 2, 3, 0):
             nc.sync.dma_start(pos_sb[r][:], (pos1, pos2, pos3, pos4)[r])
-            if r:
-                nc.sync.dma_start(out=gate_rest[r - 1][:], in_=gate[r, 0:P, 0:TV])
-            else:
-                nc.sync.dma_start(out=gate_first[:], in_=gate[0, 0:P, :])
-
-        for c in range(CHUNKS):
-            nc.tensor.transpose(banks[7][:, c * P : (c + 1) * P], gate_rows[:, c * P : (c + 1) * P], ident[:])
-        by_chunk = banks[7][:, : CHUNKS * P].rearrange("p (c r) -> p c r", r=P)
-        nc.scalar.copy(gate_col1[:], by_chunk[:, :, 0])
-        nc.scalar.copy(gate_col23[:], by_chunk[:, :, 1:3])
+        nc.sync.dma_start(out=gate_first[:, :TV], in_=gate[0, 0:P, :TV])
+        for r in range(1, TOP):
+            nc.sync.dma_start(out=gate_rest[r - 1][:], in_=gate[r, 0:P, :TV])
+        nc.sync.dma_start(out=gate_first[:, TV:], in_=gate[0, 0:P, TV:])
+        load_words(w2[1], w2_words, 4, 8)
 
         def interleave(c, a, b, engine):
             copy = nc.vector.tensor_copy if engine == "vector" else nc.scalar.copy
@@ -268,74 +260,84 @@ def tile_moe_ecr_glu_relu_kernel(
         def add_turned(dst, src, start, stop):
             nc.tensor.matmul(dst, src, ident[:], start=start, stop=stop, is_transpose=True)
 
-        def store(h0, h1, a, b):
-            nc.sync.dma_start(out=out[h0 * P : h1 * P, a:b].rearrange("(h p) t -> p h t", p=P), in_=res[:, h0:h1, a:b])
-
         sum_banks = [banks[5], banks[4]]
-        plain_banks = {1: (banks[3], banks[6]), 2: (banks[0], banks[1]), 3: (banks[3], banks[6])}
-        back_banks = [banks[7], banks[2]]
-        groups = [(0, 2), (2, 3)]
-        first = sb("first", [P, 2, T], F32)
+        plain_banks = {1: banks[3], 2: banks[6], 3: banks[0]}
+        back_bank = banks[1]
 
-        def gated_sum(hf):
-            for r in range(1, TOP):
-                prod = sb("prod%d%d" % (hf, r), [P, TV], F32)
-                nc.vector.tensor_tensor(prod[:], y[hf][:].indirect(offsets(r, 0, TV)), gate_rest[r - 1][:], MULT)
-                for c in range(0, TV, P):
-                    add_turned(sum_banks[hf][:, c : c + P], prod[:, c : c + P], r == 1 and c == 0, r == TOP - 1 and c == TV - P)
+        for c in range(CHUNKS):
+            nc.tensor.transpose(banks[3][:, c * P : (c + 1) * P], gate_rows[:, c * P : (c + 1) * P], ident[:])
+        by_chunk = banks[3][:, : CHUNKS * P].rearrange("p (c r) -> p c r", r=P)
+        nc.scalar.copy(gate_col1[:], by_chunk[:, :, 0])
+        nc.scalar.copy(gate_col23[:], by_chunk[:, :, 1:3])
+
+        def gated(dst, hf, r, a, b):
+            factor = gate_rest[r - 1][:, a:b] if r else gate_first[:, a:b]
+            nc.vector.tensor_tensor(dst, y[hf][:].indirect(offsets(r, a, b)), factor, MULT)
+
+        def gated_term(prod, hf, r):
+            gated(prod, hf, r, 0, TV)
+            for c in range(0, TV, P):
+                add_turned(sum_banks[hf][:, c : c + P], prod[:, c : c + P], r == hf and c == 0, r == TOP - 1 and c == TV - P)
 
         def gated_back(hf):
-            nc.scalar.copy(turned[hf][:], sum_banks[hf][:, :TV])
+            turned = sb("turned%d" % hf, [P, TV], F32, ("gate_col1", "gate_col23")[hf])
+            nc.scalar.copy(turned[:], sum_banks[hf][:])
             for c in range(0, TV, P):
-                nc.tensor.transpose(sum_banks[hf][:, c : c + P], turned[hf][:, c : c + P], ident[:])
+                nc.tensor.transpose(sum_banks[hf][:, c : c + P], turned[:, c : c + P], ident[:])
 
-        def plain_fetch(r):
-            got = []
-            for hf in range(2):
-                t = sb("plain%d%d" % (hf, r), [P, T - TV], F32, "gate_col1" if (r, hf) == (3, 0) else None)
-                nc.scalar.activation(t[:], y[hf][:].indirect(offsets(r, TV, T)), COPY)
-                got.append(t)
-            for g, (c0, c1) in enumerate(groups):
-                for c in range(c0, c1):
-                    for hf in range(2):
-                        col = (2 * (c - c0) + hf) * P
-                        nc.tensor.transpose(plain_banks[r][g][:, col : col + P], got[hf][:, c * P : (c + 1) * P], ident[:])
+        def plain_fetch(hf, r):
+            got = sb("plain%d%d" % (hf, r), [P, T - TV], F32)
+            nc.scalar.activation(got[:], y[hf][:].indirect(offsets(r, TV, T)), COPY)
+            for c in range(CHUNKS):
+                col = (2 * c + hf) * P
+                nc.tensor.transpose(plain_banks[r][:, col : col + P], got[:, c * P : (c + 1) * P], ident[:])
 
         def plain_back(r):
             scaled = sb("scaled%d" % r, [P, CHUNKS, 2 * P], F32)
-            for g, (c0, c1) in enumerate(groups):
-                for c in range(c0, c1):
-                    col = 2 * (c - c0) * P
-                    factor = gate_col1[:, c : c + 1] if r == 1 else gate_col23[:, c, r - 2 : r - 1]
-                    nc.scalar.activation(scaled[:, c, :], plain_banks[r][g][:, col : col + 2 * P], COPY, scale=factor)
-                for c in range(c0, c1):
-                    for hf in range(2):
-                        col = (hf * (c1 - c0) + c - c0) * P
-                        add_turned(
-                            back_banks[g][:, col : col + P],
-                            scaled[:, c, hf * P : (hf + 1) * P],
-                            r == 1 and c == c0 and hf == 0,
-                            r == TOP - 1 and c == c1 - 1 and hf == 1,
-                        )
+            for c in range(CHUNKS):
+                factor = gate_col1[:, c : c + 1] if r == 1 else gate_col23[:, c, r - 2 : r - 1]
+                nc.scalar.activation(scaled[:, c, :], plain_banks[r][:, 2 * c * P : 2 * (c + 1) * P], COPY, scale=factor)
+                for hf in range(2):
+                    col = (hf * CHUNKS + c) * P
+                    add_turned(
+                        back_bank[:, col : col + P],
+                        scaled[:, c, hf * P : (hf + 1) * P],
+                        r == 1 and c == 0 and hf == 0,
+                        r == TOP - 1 and c == CHUNKS - 1 and hf == 1,
+                    )
 
-        gated_sum(0)
-        plain_fetch(1)
-        gated_sum(1)
-        plain_fetch(2)
+        prods = [sb("prod%d" % r, [P, TV], F32) for r in range(TOP)]
+        gated_term(prods[0][:], 0, 0)
+        plain_fetch(0, 1)
+        gated_term(prods[1][:], 0, 1)
+        plain_fetch(1, 1)
+        gated_term(prods[2][:], 0, 2)
+        plain_fetch(0, 2)
+        plain_fetch(1, 2)
+        gated_term(prods[3][:], 0, 3)
+        plain_fetch(0, 3)
+        plain_fetch(1, 3)
+        later = sb("later", [P, 3 * TV + T], F32)
+        first1 = later[:, 3 * TV :]
+        gated_term(later[:, 0:TV], 1, 1)
         plain_back(1)
-        plain_fetch(3)
-        plain_back(2)
         gated_back(0)
-        gated_back(1)
+        gated_term(later[:, TV : 2 * TV], 1, 2)
+        plain_back(2)
         plain_back(3)
-        for hf in range(2):
-            nc.vector.tensor_tensor(first[:, hf, :], y[hf][:].indirect(offsets(0, 0, T)), gate_first[:], MULT)
-        for hf in range(2):
-            nc.vector.tensor_tensor(res[:, hf, :TV], sum_banks[hf][:, :TV], first[:, hf, :TV], ADD)
-            store(hf, hf + 1, 0, TV)
-        for g, (c0, c1) in enumerate(groups):
-            a, b = TV + c0 * P, TV + c1 * P
-            nc.vector.tensor_tensor(
-                res[:, :, a:b], back_banks[g][:, : 2 * (b - a)].rearrange("p (h t) -> p h t", h=2), first[:, :, a:b], ADD
-            )
-            store(0, 2, a, b)
+        gated_term(later[:, 2 * TV : 3 * TV], 1, 3)
+        res0 = sb("res0", [P, TV], F32)
+        nc.scalar.copy(res0[:], sum_banks[0][:])
+        nc.sync.dma_start(out=out[0:P, :TV], in_=res0[:])
+        gated_back(1)
+        first_s0 = sb("first_s0", [P, T - TV], F32)
+        gated(first_s0[:], 0, 0, TV, T)
+        gated(first1, 1, 0, 0, T)
+        res_s = sb("res_s", [P, 2, T - TV], F32)
+        for hf, first in ((0, first_s0[:]), (1, first1[:, TV:])):
+            nc.vector.tensor_tensor(res_s[:, hf, :], back_bank[:, hf * (T - TV) : (hf + 1) * (T - TV)], first, ADD)
+        nc.sync.dma_start(out=out[:, TV:].rearrange("(h p) t -> p h t", p=P), in_=res_s[:])
+        for a, b in ((0, TV // 2), (TV // 2, TV)):
+            res1 = sb("res1_%d" % a, [P, b - a], F32)
+            nc.vector.tensor_tensor(res1[:], sum_banks[1][:, a:b], first1[:, a:b], ADD)
+            nc.sync.dma_start(out=out[P:, a:b], in_=res1[:])

@@ -61,8 +61,7 @@ def tile_moe_ecr_glu_relu_kernel(
         gate_first = sb("gate_first", [P, T], F32)
         gate_rest = [sb("gate_rest%d" % r, [P, TV], F32) for r in range(1, TOP)]
         gate_rows = sb("gate_rows", [P, T - TV], F32)
-        gate_col1 = sb("gate_col1", [P, CHUNKS], F32)
-        gate_col23 = sb("gate_col23", [P, CHUNKS, 2], F32)
+        gate_cols = sb("gate_cols", [P, CHUNKS, TOP - 1], F32)
         ident = sb("ident", [P, P], F32)
         warm = sb("warm", [P, 8], F32)
         relu_a = [sb("relu_a%d" % e, [P, H], F32) for e in range(E)]
@@ -111,14 +110,15 @@ def tile_moe_ecr_glu_relu_kernel(
             load_words(w[g], src, *W1_GROUPS[g])
         load_words(w2[0], w2_words, 0, 4)
         load_scales(nc.sync, s2, w2_scales, 0, E)
-        nc.sync.dma_start(out=gate_rows[0 : TOP - 1, :], in_=gate[1:TOP, 0, TV:T])
+        load_words(w2[1], w2_words, 4, 8)
         for r in (1, 2, 3, 0):
             nc.sync.dma_start(pos_sb[r][:], (pos1, pos2, pos3, pos4)[r])
-        nc.sync.dma_start(out=gate_first[:, :TV], in_=gate[0, 0:P, :TV])
-        for r in range(1, TOP):
-            nc.sync.dma_start(out=gate_rest[r - 1][:], in_=gate[r, 0:P, :TV])
-        nc.sync.dma_start(out=gate_first[:, TV:], in_=gate[0, 0:P, TV:])
-        load_words(w2[1], w2_words, 4, 8)
+            if r:
+                nc.sync.dma_start(out=gate_rest[r - 1][:], in_=gate[r, 0:P, :TV])
+            else:
+                nc.sync.dma_start(out=gate_first[:], in_=gate[0, 0:P, :])
+            if r == 2:
+                nc.sync.dma_start(out=gate_rows[0 : TOP - 1, :], in_=gate[1:TOP, 0, TV:T])
 
         def interleave(c, a, b, engine):
             copy = nc.vector.tensor_copy if engine == "vector" else nc.scalar.copy
@@ -265,22 +265,21 @@ def tile_moe_ecr_glu_relu_kernel(
         back_bank = banks[1]
 
         for c in range(CHUNKS):
-            nc.tensor.transpose(banks[3][:, c * P : (c + 1) * P], gate_rows[:, c * P : (c + 1) * P], ident[:])
-        by_chunk = banks[3][:, : CHUNKS * P].rearrange("p (c r) -> p c r", r=P)
-        nc.scalar.copy(gate_col1[:], by_chunk[:, :, 0])
-        nc.scalar.copy(gate_col23[:], by_chunk[:, :, 1:3])
+            nc.tensor.transpose(banks[7][:, c * P : (c + 1) * P], gate_rows[:, c * P : (c + 1) * P], ident[:])
+        nc.scalar.copy(gate_cols[:], banks[7][:, : CHUNKS * P].rearrange("p (c r) -> p c r", r=P)[:, :, : TOP - 1])
 
         def gated(dst, hf, r, a, b):
             factor = gate_rest[r - 1][:, a:b] if r else gate_first[:, a:b]
             nc.vector.tensor_tensor(dst, y[hf][:].indirect(offsets(r, a, b)), factor, MULT)
 
-        def gated_term(prod, hf, r):
-            gated(prod, hf, r, 0, TV)
+        def gated_term(hf, r):
+            prod = sb("prod%d%d" % (hf, r), [P, TV], F32, "prod01" if (hf, r) == (1, 1) else None)
+            gated(prod[:], hf, r, 0, TV)
             for c in range(0, TV, P):
-                add_turned(sum_banks[hf][:, c : c + P], prod[:, c : c + P], r == hf and c == 0, r == TOP - 1 and c == TV - P)
+                add_turned(sum_banks[hf][:, c : c + P], prod[:, c : c + P], r == 1 and c == 0, r == TOP - 1 and c == TV - P)
 
         def gated_back(hf):
-            turned = sb("turned%d" % hf, [P, TV], F32, ("gate_col1", "gate_col23")[hf])
+            turned = sb("turned%d" % hf, [P, TV], F32)
             nc.scalar.copy(turned[:], sum_banks[hf][:])
             for c in range(0, TV, P):
                 nc.tensor.transpose(sum_banks[hf][:, c : c + P], turned[:, c : c + P], ident[:])
@@ -295,7 +294,7 @@ def tile_moe_ecr_glu_relu_kernel(
         def plain_back(r):
             scaled = sb("scaled%d" % r, [P, CHUNKS, 2 * P], F32)
             for c in range(CHUNKS):
-                factor = gate_col1[:, c : c + 1] if r == 1 else gate_col23[:, c, r - 2 : r - 1]
+                factor = gate_cols[:, c, r - 1 : r]
                 nc.scalar.activation(scaled[:, c, :], plain_banks[r][:, 2 * c * P : 2 * (c + 1) * P], COPY, scale=factor)
                 for hf in range(2):
                     col = (hf * CHUNKS + c) * P
@@ -306,38 +305,35 @@ def tile_moe_ecr_glu_relu_kernel(
                         r == TOP - 1 and c == CHUNKS - 1 and hf == 1,
                     )
 
-        prods = [sb("prod%d" % r, [P, TV], F32) for r in range(TOP)]
-        gated_term(prods[0][:], 0, 0)
+        gated_term(0, 1)
         plain_fetch(0, 1)
-        gated_term(prods[1][:], 0, 1)
+        gated_term(0, 2)
         plain_fetch(1, 1)
-        gated_term(prods[2][:], 0, 2)
+        gated_term(1, 1)
         plain_fetch(0, 2)
+        gated_term(1, 2)
         plain_fetch(1, 2)
-        gated_term(prods[3][:], 0, 3)
-        plain_fetch(0, 3)
-        plain_fetch(1, 3)
-        later = sb("later", [P, 3 * TV + T], F32)
-        first1 = later[:, 3 * TV :]
-        gated_term(later[:, 0:TV], 1, 1)
         plain_back(1)
-        gated_back(0)
-        gated_term(later[:, TV : 2 * TV], 1, 2)
+        for hf in range(2):
+            gated_term(hf, 3)
+            plain_fetch(hf, 3)
         plain_back(2)
+        gated_back(0)
         plain_back(3)
-        gated_term(later[:, 2 * TV : 3 * TV], 1, 3)
-        res0 = sb("res0", [P, TV], F32)
-        nc.scalar.copy(res0[:], sum_banks[0][:])
-        nc.sync.dma_start(out=out[0:P, :TV], in_=res0[:])
         gated_back(1)
-        first_s0 = sb("first_s0", [P, T - TV], F32)
-        gated(first_s0[:], 0, 0, TV, T)
-        gated(first1, 1, 0, 0, T)
+        half = TV // 2
+        first = sb("first", [P, 2, T], F32)
+        gated(first[:, 0, :], 0, 0, 0, T)
+        gated(first[:, 1, half:], 1, 0, half, T)
+        res0 = sb("res0", [P, TV], F32)
+        nc.vector.tensor_tensor(res0[:], sum_banks[0][:], first[:, 0, :TV], ADD)
+        nc.sync.dma_start(out=out[0:P, :TV], in_=res0[:])
+        last = sb("last", [P, half], F32, "turned0")
+        gated(last[:], 1, 0, 0, half)
         res_s = sb("res_s", [P, 2, T - TV], F32)
-        for hf, first in ((0, first_s0[:]), (1, first1[:, TV:])):
-            nc.vector.tensor_tensor(res_s[:, hf, :], back_bank[:, hf * (T - TV) : (hf + 1) * (T - TV)], first, ADD)
+        nc.vector.tensor_tensor(res_s[:], back_bank[:].rearrange("p (h t) -> p h t", h=2), first[:, :, TV:], ADD)
         nc.sync.dma_start(out=out[:, TV:].rearrange("(h p) t -> p h t", p=P), in_=res_s[:])
-        for a, b in ((0, TV // 2), (TV // 2, TV)):
-            res1 = sb("res1_%d" % a, [P, b - a], F32)
-            nc.vector.tensor_tensor(res1[:], sum_banks[1][:, a:b], first1[:, a:b], ADD)
-            nc.sync.dma_start(out=out[P:, a:b], in_=res1[:])
+        for a, term in ((half, first[:, 1, half:TV]), (0, last[:])):
+            res1 = sb("res1_%d" % a, [P, half], F32)
+            nc.vector.tensor_tensor(res1[:], sum_banks[1][:, a : a + half], term, ADD)
+            nc.sync.dma_start(out=out[P:, a : a + half], in_=res1[:])

@@ -263,6 +263,8 @@ def tile_moe_ecr_glu_relu_kernel(
         sum_banks = [banks[5], banks[4]]
         plain_banks = {1: banks[3], 2: banks[6], 3: banks[0]}
         back_bank = banks[1]
+        half = TV // 2
+        turn_from = (0, half)
 
         for c in range(CHUNKS):
             nc.tensor.transpose(banks[7][:, c * P : (c + 1) * P], gate_rows[:, c * P : (c + 1) * P], ident[:])
@@ -275,13 +277,16 @@ def tile_moe_ecr_glu_relu_kernel(
         def gated_term(hf, r):
             prod = sb("prod%d%d" % (hf, r), [P, TV], F32, "prod01" if (hf, r) == (1, 1) else None)
             gated(prod[:], hf, r, 0, TV)
-            for c in range(0, TV, P):
-                add_turned(sum_banks[hf][:, c : c + P], prod[:, c : c + P], r == 1 and c == 0, r == TOP - 1 and c == TV - P)
+            for c in range(turn_from[hf], TV, P):
+                add_turned(
+                    sum_banks[hf][:, c : c + P], prod[:, c : c + P], r == 1 and c == turn_from[hf], r == TOP - 1 and c == TV - P
+                )
+            return prod
 
         def gated_back(hf):
             turned = sb("turned%d" % hf, [P, TV], F32)
-            nc.scalar.copy(turned[:], sum_banks[hf][:])
-            for c in range(0, TV, P):
+            nc.scalar.copy(turned[:, turn_from[hf] :], sum_banks[hf][:, turn_from[hf] :])
+            for c in range(turn_from[hf], TV, P):
                 nc.tensor.transpose(sum_banks[hf][:, c : c + P], turned[:, c : c + P], ident[:])
 
         def plain_fetch(hf, r):
@@ -309,31 +314,33 @@ def tile_moe_ecr_glu_relu_kernel(
         plain_fetch(0, 1)
         gated_term(0, 2)
         plain_fetch(1, 1)
-        gated_term(1, 1)
+        p1 = gated_term(1, 1)
         plain_fetch(0, 2)
-        gated_term(1, 2)
         plain_fetch(1, 2)
+        p2 = gated_term(1, 2)
         plain_back(1)
-        for hf in range(2):
-            gated_term(hf, 3)
-            plain_fetch(hf, 3)
+        gated_term(0, 3)
+        plain_fetch(0, 3)
+        p3 = gated_term(1, 3)
+        plain_fetch(1, 3)
         plain_back(2)
         gated_back(0)
         plain_back(3)
         gated_back(1)
-        half = TV // 2
+        sum12 = sb("sum12", [P, half], F32, "prod03")
+        nc.vector.tensor_tensor(sum12[:], p1[:, :half], p2[:, :half], ADD)
         first = sb("first", [P, 2, T], F32)
-        gated(first[:, 0, :], 0, 0, 0, T)
-        gated(first[:, 1, half:], 1, 0, half, T)
+        for hf in (1, 0):
+            gated(first[:, hf, :], hf, 0, 0, T)
+        nc.vector.tensor_tensor(p3[:, :half], p3[:, :half], first[:, 1, :half], ADD)
         res0 = sb("res0", [P, TV], F32)
         nc.vector.tensor_tensor(res0[:], sum_banks[0][:], first[:, 0, :TV], ADD)
         nc.sync.dma_start(out=out[0:P, :TV], in_=res0[:])
-        last = sb("last", [P, half], F32, "turned0")
-        gated(last[:], 1, 0, 0, half)
+        nc.vector.tensor_tensor(sum12[:], sum12[:], p3[:, :half], ADD)
+        nc.sync.dma_start(out=out[P:, :half], in_=sum12[:])
         res_s = sb("res_s", [P, 2, T - TV], F32)
         nc.vector.tensor_tensor(res_s[:], back_bank[:].rearrange("p (h t) -> p h t", h=2), first[:, :, TV:], ADD)
         nc.sync.dma_start(out=out[:, TV:].rearrange("(h p) t -> p h t", p=P), in_=res_s[:])
-        for a, term in ((half, first[:, 1, half:TV]), (0, last[:])):
-            res1 = sb("res1_%d" % a, [P, half], F32)
-            nc.vector.tensor_tensor(res1[:], sum_banks[1][:, a : a + half], term, ADD)
-            nc.sync.dma_start(out=out[P:, a : a + half], in_=res1[:])
+        res1 = sb("res1", [P, half], F32)
+        nc.vector.tensor_tensor(res1[:], sum_banks[1][:, half:], first[:, 1, half:TV], ADD)
+        nc.sync.dma_start(out=out[P:, half:TV], in_=res1[:])

@@ -117,7 +117,7 @@ def tile_moe_ecr_glu_relu_kernel(
                 nc.sync.dma_start(out=gate_rest[r - 1][:], in_=gate[r, 0:P, :TV])
             else:
                 nc.sync.dma_start(out=gate_first[:], in_=gate[0, 0:P, :])
-            if r == 2:
+            if r == 3:
                 nc.sync.dma_start(out=gate_rows[0 : TOP - 1, :], in_=gate[1:TOP, 0, TV:T])
 
         def interleave(c, a, b, engine):
@@ -262,7 +262,7 @@ def tile_moe_ecr_glu_relu_kernel(
 
         sum_banks = [banks[5], banks[4]]
         plain_banks = {1: banks[3], 2: banks[6], 3: banks[0]}
-        back_bank = banks[1]
+        back_banks = [banks[1], banks[1]]
         half = TV // 2
         turn_from = (0, half)
 
@@ -275,7 +275,7 @@ def tile_moe_ecr_glu_relu_kernel(
             nc.vector.tensor_tensor(dst, y[hf][:].indirect(offsets(r, a, b)), factor, MULT)
 
         def gated_term(hf, r):
-            prod = sb("prod%d%d" % (hf, r), [P, TV], F32, "prod01" if (hf, r) == (1, 1) else None)
+            prod = sb("prod%d%d" % (hf, r), [P, TV], F32, None)
             gated(prod[:], hf, r, 0, TV)
             for c in range(turn_from[hf], TV, P):
                 add_turned(
@@ -302,45 +302,50 @@ def tile_moe_ecr_glu_relu_kernel(
                 factor = gate_cols[:, c, r - 1 : r]
                 nc.scalar.activation(scaled[:, c, :], plain_banks[r][:, 2 * c * P : 2 * (c + 1) * P], COPY, scale=factor)
                 for hf in range(2):
-                    col = (hf * CHUNKS + c) * P
                     add_turned(
-                        back_bank[:, col : col + P],
+                        back_banks[c][:, (hf * CHUNKS + c) * P : (hf * CHUNKS + c + 1) * P],
                         scaled[:, c, hf * P : (hf + 1) * P],
-                        r == 1 and c == 0 and hf == 0,
-                        r == TOP - 1 and c == CHUNKS - 1 and hf == 1,
+                        r == 1 and hf == 0 and c == 0,
+                        r == TOP - 1 and hf == 1 and c == CHUNKS - 1,
                     )
+
+        first = sb("first", [P, 2, T], F32)
+
+        def close(name, rows, a, b, src0, src1):
+            res = sb(name, [P, b - a], F32)
+            nc.vector.tensor_tensor(res[:], src0, src1, ADD)
+            nc.sync.dma_start(out=out[rows, a:b], in_=res[:])
+
+        def close_plain(hf):
+            w = T - TV
+            close("res_s%d" % hf, slice(hf * P, (hf + 1) * P), TV, T, back_banks[0][:, hf * w : (hf + 1) * w], first[:, hf, TV:])
 
         gated_term(0, 1)
         plain_fetch(0, 1)
         gated_term(0, 2)
         plain_fetch(1, 1)
-        p1 = gated_term(1, 1)
+        gated_term(0, 3)
         plain_fetch(0, 2)
+        p1 = gated_term(1, 1)
+        gated_back(0)
         plain_fetch(1, 2)
         p2 = gated_term(1, 2)
         plain_back(1)
-        gated_term(0, 3)
-        plain_fetch(0, 3)
         p3 = gated_term(1, 3)
+        plain_fetch(0, 3)
+        gated(first[:, 0, :TV], 0, 0, 0, TV)
         plain_fetch(1, 3)
-        plain_back(2)
-        gated_back(0)
-        plain_back(3)
-        gated_back(1)
-        sum12 = sb("sum12", [P, half], F32, "prod03")
+        sum12 = sb("sum12", [P, half], F32)
         nc.vector.tensor_tensor(sum12[:], p1[:, :half], p2[:, :half], ADD)
-        first = sb("first", [P, 2, T], F32)
-        for hf in (1, 0):
-            gated(first[:, hf, :], hf, 0, 0, T)
+        close("res0", slice(0, P), 0, TV, sum_banks[0][:], first[:, 0, :TV])
+        gated_back(1)
+        plain_back(2)
+        gated(first[:, 1, :TV], 1, 0, 0, TV)
+        plain_back(3)
+        gated(first[:, 0, TV:], 0, 0, TV, T)
         nc.vector.tensor_tensor(p3[:, :half], p3[:, :half], first[:, 1, :half], ADD)
-        res0 = sb("res0", [P, TV], F32)
-        nc.vector.tensor_tensor(res0[:], sum_banks[0][:], first[:, 0, :TV], ADD)
-        nc.sync.dma_start(out=out[0:P, :TV], in_=res0[:])
-        nc.vector.tensor_tensor(sum12[:], sum12[:], p3[:, :half], ADD)
-        nc.sync.dma_start(out=out[P:, :half], in_=sum12[:])
-        res_s = sb("res_s", [P, 2, T - TV], F32)
-        nc.vector.tensor_tensor(res_s[:], back_bank[:].rearrange("p (h t) -> p h t", h=2), first[:, :, TV:], ADD)
-        nc.sync.dma_start(out=out[:, TV:].rearrange("(h p) t -> p h t", p=P), in_=res_s[:])
-        res1 = sb("res1", [P, half], F32)
-        nc.vector.tensor_tensor(res1[:], sum_banks[1][:, half:], first[:, 1, half:TV], ADD)
-        nc.sync.dma_start(out=out[P:, half:TV], in_=res1[:])
+        close("res1", slice(P, 2 * P), half, TV, sum_banks[1][:, half:], first[:, 1, half:TV])
+        close("res2", slice(P, 2 * P), 0, half, sum12[:], p3[:, :half])
+        gated(first[:, 1, TV:], 1, 0, TV, T)
+        close_plain(0)
+        close_plain(1)

@@ -109,7 +109,6 @@ def tile_moe_ecr_glu_relu_kernel(
         for w, src, g in ((w3, w3_words, 0), (w1, w1_words, 2), (w3, w3_words, 1), (w1, w1_words, 3), (w3, w3_words, 2), (w3, w3_words, 3)):
             load_words(w[g], src, *W1_GROUPS[g])
         load_words(w2[0], w2_words, 0, 4)
-        load_scales(nc.sync, s2, w2_scales, 0, E)
         load_words(w2[1], w2_words, 4, 8)
         for r in (1, 2, 3, 0):
             nc.sync.dma_start(pos_sb[r][:], (pos1, pos2, pos3, pos4)[r])
@@ -178,7 +177,11 @@ def tile_moe_ecr_glu_relu_kernel(
             return ap.rearrange("s (u m d) -> s u m d", u=2, d=2)
 
         def relu(e):
-            nc.scalar.activation(in_order(relu_a[e][:]), by_word(bank_a[e][:]), RELU)
+            if e == 0:
+                nc.scalar.activation(in_order(relu_a[e][:]), by_word(bank_a[e][:]), RELU, bias=s2[:, 0, 0:4].bitcast(F32))
+                load_scales(nc.gpsimd, s2, w2_scales, 0, E)
+            else:
+                nc.scalar.activation(in_order(relu_a[e][:]), by_word(bank_a[e][:]), RELU)
 
         def product(e):
             nc.vector.tensor_tensor(in_order(h_rows[e][:]), by_word(bank_b[e][:]), in_order(relu_a[e][:]), MULT)

@@ -27,8 +27,11 @@ X_CASTS = [(0, 0, 256, "vector"), (1, 256, 424, "vector"), (1, 424, 512, "scalar
 X_QUANT = 256
 W1_GROUPS = [(0, 2), (2, 4), (4, 6), (6, 8)]
 W3_GROUPS = W1_GROUPS
-GATHER_GROUPS = [(0, 1), (1, 3), (3, 5), (5, 7), (7, 8)]
-TURN_GROUPS = [(0, 2), (2, 4), (4, 6), (6, 7), (7, 8)]
+W2_GROUPS = [(0, 6), (6, 8)]
+GATHER_GROUPS = [(0, 1), (1, 2), (2, 3), (3, 4), (4, 6), (6, 8)]
+TURN_GROUPS = [(2, 4), (4, 6), (6, 7), (0, 2), (7, 8)]
+QUANT_GROUPS = [(2, 4), (4, 6), (0, 2), (6, 8)]
+POOL_EXPERTS = 2
 TV = 512
 CHUNKS = (T - TV) // P
 
@@ -57,23 +60,26 @@ def tile_moe_ecr_glu_relu_kernel(
         s2 = sb("s2", [P, E, N], U8)
         w1 = [sb("w1_%d" % a, [P, b - a, 2 * H], U8) for a, b in W1_GROUPS]
         w3 = [sb("w3_%d" % a, [P, b - a, 2 * H], U8) for a, b in W3_GROUPS]
-        w2 = [sb("w2_%d" % h, [P, 4, 2 * N], U8) for h in range(2)]
+        w2 = [sb("w2_%d" % a, [P, b - a, 2 * N], U8) for a, b in W2_GROUPS]
         gate_first = sb("gate_first", [P, T], F32)
-        gate_rest = [sb("gate_rest%d" % r, [P, TV], F32) for r in range(1, TOP)]
+        gate_pair = sb("gate_pair", [P, 2, TV], F32)
+        gate_last = sb("gate_last", [P, TV], F32)
+        gate_rest = [gate_pair[:, 0, :], gate_pair[:, 1, :], gate_last[:]]
         gate_rows = sb("gate_rows", [P, T - TV], F32)
         gate_cols = sb("gate_cols", [P, CHUNKS, TOP - 1], F32)
         ident = sb("ident", [P, P], F32)
         warm = sb("warm", [P, 8], F32)
         relu_a = [sb("relu_a%d" % e, [P, H], F32) for e in range(E)]
-        h_rows = [sb("h_rows%d" % e, [P, H], BF16) for e in range(E)]
-        h_cols = [sb("h_cols%d" % a, [P, (b - a) * H], BF16) for a, b in TURN_GROUPS]
-        h_scales = [sb("h_scales%d" % a, [P, (b - a) * C], U8) for a, b in TURN_GROUPS]
+        gate_b = [sb("gate_b%d" % e, [P, H], F32) for e in range(POOL_EXPERTS)]
+        h_rows = {e: sb("h_rows%d" % e, [P, H], BF16) for e in range(POOL_EXPERTS, E)}
+        h_cols = [sb("h_cols%d" % a, [P, (b - a) * H], BF16) for a, b in QUANT_GROUPS]
+        h_scales = [sb("h_scales%d" % a, [P, (b - a) * C], U8) for a, b in QUANT_GROUPS]
         y = [sb("y%d" % hf, [P, S + PAD], F32) for hf in range(2)]
 
         banks = [psum.tile([P, 512], F32, name="bank%d" % i) for i in range(8)]
         bank_a = [banks[i] for i in (0, 1, 6, 7, 0, 1, 6, 7)]
         bank_b = [banks[i] for i in (2, 3, 4, 5, 2, 3, 4, 5)]
-        bank_t = [banks[i] for i in (6, 7, 0, 1, 6)]
+        bank_t = [banks[i] for i in (6, 7, 0, 4, 5)]
 
         def zero(eng, t):
             eng.memset(t[:].rearrange("p e n -> p (e n)").bitcast(I32), 0)
@@ -106,18 +112,18 @@ def tile_moe_ecr_glu_relu_kernel(
         load_words(w1[0], w1_words, *W1_GROUPS[0])
         load_words(w1[1], w1_words, *W1_GROUPS[1])
         load_scales(nc.sync, s3, w3_scales, 0, E)
-        for w, src, g in ((w3, w3_words, 0), (w1, w1_words, 2), (w3, w3_words, 1), (w1, w1_words, 3), (w3, w3_words, 2), (w3, w3_words, 3)):
+        for w, src, g in ((w3, w3_words, 0), (w3, w3_words, 1), (w1, w1_words, 2), (w3, w3_words, 2), (w1, w1_words, 3), (w3, w3_words, 3)):
             load_words(w[g], src, *W1_GROUPS[g])
-        load_words(w2[0], w2_words, 0, 4)
-        load_words(w2[1], w2_words, 4, 8)
-        for r in (1, 2, 3, 0):
+        load_scales(nc.sync, s2, w2_scales, 0, E)
+        load_words(w2[0], w2_words, *W2_GROUPS[0])
+        for r in (1, 2, 3):
             nc.sync.dma_start(pos_sb[r][:], (pos1, pos2, pos3, pos4)[r])
-            if r:
-                nc.sync.dma_start(out=gate_rest[r - 1][:], in_=gate[r, 0:P, :TV])
-            else:
-                nc.sync.dma_start(out=gate_first[:], in_=gate[0, 0:P, :])
-            if r == 3:
-                nc.sync.dma_start(out=gate_rows[0 : TOP - 1, :], in_=gate[1:TOP, 0, TV:T])
+        nc.sync.dma_start(out=gate_pair[:], in_=gate[1:3, 0:P, :TV].rearrange("r p t -> p r t"))
+        load_words(w2[1], w2_words, *W2_GROUPS[1])
+        nc.sync.dma_start(out=gate_last[:], in_=gate[3, 0:P, :TV])
+        nc.sync.dma_start(out=gate_rows[0 : TOP - 1, :], in_=gate[1:TOP, 0, TV:T])
+        nc.sync.dma_start(pos_sb[0][:], pos1)
+        nc.sync.dma_start(out=gate_first[:], in_=gate[0, 0:P, :])
 
         def interleave(c, a, b, engine):
             copy = nc.vector.tensor_copy if engine == "vector" else nc.scalar.copy
@@ -144,8 +150,8 @@ def tile_moe_ecr_glu_relu_kernel(
 
         def gather_tokens(a, b):
             lst = offs_sb[:, a * C // 16 : b * C // 16]
-            nc.vector.tensor_copy(g_words[:, a * C : b * C], x_words[:].indirect(lst))
             nc.vector.tensor_copy(g_scales[:, a * C : b * C], x_scales[:].indirect(lst))
+            nc.vector.tensor_copy(g_words[:, a * C : b * C], x_words[:].indirect(lst))
 
         def group_of(groups, e):
             return [i for i, (a, b) in enumerate(groups) if a <= e < b][0]
@@ -177,85 +183,98 @@ def tile_moe_ecr_glu_relu_kernel(
             return ap.rearrange("s (u m d) -> s u m d", u=2, d=2)
 
         def relu(e):
-            if e == 0:
-                nc.scalar.activation(in_order(relu_a[e][:]), by_word(bank_a[e][:]), RELU, bias=s2[:, 0, 0:4].bitcast(F32))
-                load_scales(nc.gpsimd, s2, w2_scales, 0, E)
-            else:
-                nc.scalar.activation(in_order(relu_a[e][:]), by_word(bank_a[e][:]), RELU)
+            nc.scalar.activation(in_order(relu_a[e][:]), by_word(bank_a[e][:]), RELU)
 
         def product(e):
             nc.vector.tensor_tensor(in_order(h_rows[e][:]), by_word(bank_b[e][:]), in_order(relu_a[e][:]), MULT)
 
-        def turn(g):
+        def turn(g, copy=nc.scalar.copy):
             a, b = TURN_GROUPS[g]
             bank = bank_t[g]
             for e in range(a, b):
-                words = h_rows[e][:].bitcast(F32)
+                words = h_rows[e][:, :].bitcast(F32)
                 for u in range(2):
                     c = (2 * (e - a) + u) * P
                     nc.tensor.transpose(bank[:, c : c + P], words[:, u * P : (u + 1) * P], ident[:])
-            nc.scalar.copy(
-                h_cols[g][:].bitcast(F32).rearrange("p (e s u) -> p e s u", u=2, s=C),
+            q = group_of(QUANT_GROUPS, a)
+            first_col = (a - QUANT_GROUPS[q][0]) * H
+            copy(
+                h_cols[q][:, first_col : first_col + (b - a) * H].bitcast(F32).rearrange("p (e s u) -> p e s u", u=2, s=C),
                 bank[:, : (b - a) * 2 * P].rearrange("p (e u s) -> p e s u", u=2, s=C),
             )
 
-        def quantise_h(g):
-            a, b = TURN_GROUPS[g]
+        def quantise_h(q):
+            a, b = QUANT_GROUPS[q]
             nc.vector.quantize_mx(
                 out=h_words[:, a * C : b * C].bitcast(FP8X4),
-                scales=h_scales[g][:],
-                in_=h_cols[g][:],
+                scales=h_scales[q][:],
+                in_=h_cols[q][:],
             )
 
-        def second_layer(hf, a, b, bank, copy=nc.scalar.copy):
-            for e in range(a, b):
-                g = group_of(TURN_GROUPS, e)
-                cols = slice((e - TURN_GROUPS[g][0]) * C, (e - TURN_GROUPS[g][0] + 1) * C)
+        def second_layer(hf, experts, bank):
+            for e in experts:
+                n = sorted(experts).index(e)
+                q, g = group_of(QUANT_GROUPS, e), group_of(W2_GROUPS, e)
+                cols = slice((e - QUANT_GROUPS[q][0]) * C, (e - QUANT_GROUPS[q][0] + 1) * C)
                 nc.tensor.matmul_mx(
-                    out=bank[:, (e - a) * C : (e - a + 1) * C],
-                    lhsT=w2[e // 4][:, e % 4, hf * 2 * P : (hf + 1) * 2 * P].bitcast(FP4X4),
+                    out=bank[:, n * C : (n + 1) * C],
+                    lhsT=w2[g][:, e - W2_GROUPS[g][0], hf * 2 * P : (hf + 1) * 2 * P].bitcast(FP4X4),
                     lhsT_scale=s2[:, e, hf * P : (hf + 1) * P],
                     rhs=h_words[:, e * C : (e + 1) * C].bitcast(FP8X4),
-                    rhs_scale=h_scales[g][:, cols],
+                    rhs_scale=h_scales[q][:, cols],
                     start=True,
                     stop=True,
                 )
+
+        def results(hf, a, b, bank, copy=nc.scalar.copy):
+            second_layer(hf, range(a, b), bank)
             copy(y[hf][:, a * C : b * C], bank[:, : (b - a) * C])
 
         for a, b in GATHER_GROUPS:
             gather_tokens(a, b)
+        pool_rows = sb("pool_rows", [P, POOL_EXPERTS, H], BF16, "x_words")
+        for e in range(POOL_EXPERTS):
+            h_rows[e] = pool_rows[:, e, :]
         for e in range(4):
             up_a(e)
-        for k in range(2):
-            up_b(2 * k)
-            up_b(2 * k + 1)
-            up_a(2 * k + 4)
-            up_a(2 * k + 5)
-        for k in range(2):
-            product(2 * k)
-            up_b(2 * k + 4)
-            product(2 * k + 1)
-            up_b(2 * k + 5)
-            turn(k)
+        for e in range(POOL_EXPERTS):
+            up_b(e)
+            nc.scalar.copy(in_order(gate_b[e][:]), by_word(bank_b[e][:]))
+            nc.gpsimd.tensor_tensor(h_rows[e], gate_b[e][:], relu_a[e][:], MULT)
+        up_b(2)
+        up_b(3)
+        up_a(4)
+        up_a(5)
+        up_b(4)
+        up_b(5)
+        up_a(6)
+        up_a(7)
+        product(2)
+        up_b(6)
+        product(3)
+        up_b(7)
+        turn(0)
         product(4)
         product(5)
-        turn(2)
+        turn(1)
         product(6)
-        turn(3)
         product(7)
-        turn(4)
         h_words = sb("h_words", [P, S], U32, "relu_a7")
+        turn(2, nc.vector.tensor_copy)
+        turn(3)
         quantise_h(0)
-        second_layer(0, 0, 2, banks[0])
+        turn(4)
         quantise_h(1)
-        second_layer(0, 2, 4, banks[1])
+        results(0, 2, 6, banks[2])
         quantise_h(2)
-        second_layer(0, 4, 6, banks[7], nc.vector.tensor_copy)
+        results(0, 0, 2, banks[3])
         quantise_h(3)
-        quantise_h(4)
-        second_layer(0, 6, 8, banks[2])
-        second_layer(1, 4, 8, banks[7])
-        second_layer(1, 0, 4, banks[2])
+        results(0, 6, 8, banks[6], nc.vector.tensor_copy)
+        second_layer(1, (6, 7, 0, 1), banks[7])
+        nc.scalar.copy(
+            y[1][:, :S].rearrange("p (g c) -> p g c", c=2 * C)[:, 0:4:3, :], banks[7][:].rearrange("p (g c) -> p g c", c=2 * C)
+        )
+        results(1, 2, 6, banks[6])
 
         def offsets(r, a, b):
             return pos_sb[r][:, a // 16 : b // 16]
@@ -264,8 +283,8 @@ def tile_moe_ecr_glu_relu_kernel(
             nc.tensor.matmul(dst, src, ident[:], start=start, stop=stop, is_transpose=True)
 
         sum_banks = [banks[5], banks[4]]
-        plain_banks = {1: banks[3], 2: banks[6], 3: banks[0]}
-        back_banks = [banks[1], banks[1]]
+        plain_banks = {1: banks[3], 2: banks[0], 3: banks[1]}
+        back_banks = [banks[2], banks[2]]
         half = TV // 2
         turn_from = (0, half)
 

@@ -22,11 +22,11 @@ RELU = mybir.ActivationFunctionType.Relu
 COPY = mybir.ActivationFunctionType.Copy
 
 P = 128
-X_LOADS = [(0, 256), (256, 512), (512, 640), (640, 768)]
-X_CASTS = [(0, 0, 256, "vector"), (1, 256, 424, "vector"), (1, 424, 512, "scalar"), (2, 512, 640, "scalar"), (3, 640, 768, "vector")]
+X_LOADS = [(0, 512), (512, 768)]
+X_CASTS = [(0, 0, 256, "vector"), (0, 256, 336, "vector"), (0, 336, 512, "scalar"), (1, 512, 680, "vector"), (1, 680, 768, "scalar")]
 X_QUANT = 256
 W1_GROUPS = [(0, 2), (2, 4), (4, 6), (6, 8)]
-W3_GROUPS = W1_GROUPS
+W3_GROUPS = [(0, 2), (2, 4), (4, 6), (6, 7), (7, 8)]
 W2_GROUPS = [(0, 6), (6, 8)]
 GATHER_GROUPS = [(0, 1), (1, 2), (2, 3), (3, 4), (4, 6), (6, 8)]
 TURN_GROUPS = [(2, 4), (4, 6), (6, 7), (0, 2), (7, 8)]
@@ -112,8 +112,11 @@ def tile_moe_ecr_glu_relu_kernel(
         load_words(w1[0], w1_words, *W1_GROUPS[0])
         load_words(w1[1], w1_words, *W1_GROUPS[1])
         load_scales(nc.sync, s3, w3_scales, 0, E)
-        for w, src, g in ((w3, w3_words, 0), (w3, w3_words, 1), (w1, w1_words, 2), (w3, w3_words, 2), (w1, w1_words, 3), (w3, w3_words, 3)):
+        for w, src, g in ((w3, w3_words, 0), (w3, w3_words, 1), (w1, w1_words, 2), (w3, w3_words, 2)):
             load_words(w[g], src, *W1_GROUPS[g])
+        load_words(w3[3], w3_words, *W3_GROUPS[3])
+        load_words(w1[3], w1_words, *W1_GROUPS[3])
+        load_words(w3[4], w3_words, *W3_GROUPS[4])
         load_scales(nc.sync, s2, w2_scales, 0, E)
         load_words(w2[0], w2_words, *W2_GROUPS[0])
         for r in (1, 2, 3):
@@ -143,10 +146,8 @@ def tile_moe_ecr_glu_relu_kernel(
 
         for cast in X_CASTS:
             interleave(*cast)
-            if cast[0] < 2 and cast[2] == X_LOADS[cast[0]][1]:
-                quantise_x(*X_LOADS[cast[0]])
-        for c in (2, 3):
-            quantise_x(*X_LOADS[c])
+            if cast[2] % X_QUANT == 0:
+                quantise_x(cast[2] - X_QUANT, cast[2])
 
         def gather_tokens(a, b):
             lst = offs_sb[:, a * C // 16 : b * C // 16]
@@ -247,10 +248,10 @@ def tile_moe_ecr_glu_relu_kernel(
         up_a(5)
         up_b(4)
         up_b(5)
-        up_a(6)
-        up_a(7)
         product(2)
         up_b(6)
+        up_a(6)
+        up_a(7)
         product(3)
         up_b(7)
         turn(0)

@@ -23,14 +23,14 @@ COPY = mybir.ActivationFunctionType.Copy
 
 P = 128
 X_LOADS = [(0, 512), (512, 768)]
-X_CASTS = [(0, 0, 256, "vector"), (0, 256, 336, "vector"), (0, 336, 512, "scalar"), (1, 512, 680, "vector"), (1, 680, 768, "scalar")]
+X_CASTS = [(0, 0, 128, "vector"), (0, 128, 256, "vector"), (0, 256, 512, "scalar"), (1, 512, 680, "vector"), (1, 680, 768, "scalar")]
 X_QUANT = 256
 W1_GROUPS = [(0, 2), (2, 4), (4, 6), (6, 8)]
 W3_GROUPS = [(0, 2), (2, 4), (4, 6), (6, 7), (7, 8)]
 W2_GROUPS = [(0, 6), (6, 8)]
 GATHER_GROUPS = [(0, 1), (1, 2), (2, 3), (3, 4), (4, 6), (6, 8)]
-TURN_GROUPS = [(2, 4), (4, 6), (6, 7), (0, 2), (7, 8)]
-QUANT_GROUPS = [(2, 4), (4, 6), (0, 2), (6, 8)]
+TURN_GROUPS = [(2, 4), (4, 6), (0, 2), (6, 7), (7, 8)]
+QUANT_GROUPS = [(2, 4), (4, 6), (0, 2), (6, 7), (7, 8)]
 POOL_EXPERTS = 2
 TV = 512
 CHUNKS = (T - TV) // P
@@ -77,9 +77,9 @@ def tile_moe_ecr_glu_relu_kernel(
         y = [sb("y%d" % hf, [P, S + PAD], F32) for hf in range(2)]
 
         banks = [psum.tile([P, 512], F32, name="bank%d" % i) for i in range(8)]
-        bank_a = [banks[i] for i in (0, 1, 6, 7, 0, 1, 6, 7)]
-        bank_b = [banks[i] for i in (2, 3, 4, 5, 2, 3, 4, 5)]
-        bank_t = [banks[i] for i in (6, 7, 0, 4, 5)]
+        bank_a = [banks[i] for i in (0, 1, 6, 7, 0, 1, 7, 4)]
+        bank_b = [banks[i] for i in (2, 3, 4, 5, 2, 3, 6, 5)]
+        bank_t = [banks[i] for i in (7, 4, 6, 0, 5)]
 
         def zero(eng, t):
             eng.memset(t[:].rearrange("p e n -> p (e n)").bitcast(I32), 0)
@@ -144,10 +144,14 @@ def tile_moe_ecr_glu_relu_kernel(
                 in_=x_bf[q][:, a - q * X_QUANT : b - q * X_QUANT, :].rearrange("p w t -> p (w t)"),
             )
 
-        for cast in X_CASTS:
+        for cast in X_CASTS[:3]:
             interleave(*cast)
-            if cast[2] % X_QUANT == 0:
-                quantise_x(cast[2] - X_QUANT, cast[2])
+        quantise_x(0, 128)
+        quantise_x(128, 256)
+        for cast in X_CASTS[3:]:
+            interleave(*cast)
+        quantise_x(256, 512)
+        quantise_x(512, 768)
 
         def gather_tokens(a, b):
             lst = offs_sb[:, a * C // 16 : b * C // 16]
@@ -248,9 +252,9 @@ def tile_moe_ecr_glu_relu_kernel(
         up_a(5)
         up_b(4)
         up_b(5)
-        product(2)
         up_b(6)
         up_a(6)
+        product(2)
         up_a(7)
         product(3)
         up_b(7)
@@ -261,21 +265,23 @@ def tile_moe_ecr_glu_relu_kernel(
         product(6)
         product(7)
         h_words = sb("h_words", [P, S], U32, "relu_a7")
-        turn(2, nc.vector.tensor_copy)
-        turn(3)
+        turn(2)
         quantise_h(0)
-        turn(4)
         quantise_h(1)
+        turn(3)
+        turn(4, nc.vector.tensor_copy)
         results(0, 2, 6, banks[2])
         quantise_h(2)
         results(0, 0, 2, banks[3])
         quantise_h(3)
-        results(0, 6, 8, banks[6], nc.vector.tensor_copy)
-        second_layer(1, (6, 7, 0, 1), banks[7])
+        quantise_h(4)
+        results(0, 6, 7, banks[1], nc.vector.tensor_copy)
+        results(0, 7, 8, banks[7], nc.vector.tensor_copy)
+        second_layer(1, (7, 6, 0, 1), banks[4])
         nc.scalar.copy(
-            y[1][:, :S].rearrange("p (g c) -> p g c", c=2 * C)[:, 0:4:3, :], banks[7][:].rearrange("p (g c) -> p g c", c=2 * C)
+            y[1][:, :S].rearrange("p (g c) -> p g c", c=2 * C)[:, 0:4:3, :], banks[4][:].rearrange("p (g c) -> p g c", c=2 * C)
         )
-        results(1, 2, 6, banks[6])
+        results(1, 2, 6, banks[7])
 
         def offsets(r, a, b):
             return pos_sb[r][:, a // 16 : b // 16]
@@ -283,15 +289,15 @@ def tile_moe_ecr_glu_relu_kernel(
         def add_turned(dst, src, start, stop):
             nc.tensor.matmul(dst, src, ident[:], start=start, stop=stop, is_transpose=True)
 
-        sum_banks = [banks[5], banks[4]]
+        sum_banks = [banks[5], banks[6]]
         plain_banks = {1: banks[3], 2: banks[0], 3: banks[1]}
         back_banks = [banks[2], banks[2]]
         half = TV // 2
         turn_from = (0, half)
 
         for c in range(CHUNKS):
-            nc.tensor.transpose(banks[7][:, c * P : (c + 1) * P], gate_rows[:, c * P : (c + 1) * P], ident[:])
-        nc.scalar.copy(gate_cols[:], banks[7][:, : CHUNKS * P].rearrange("p (c r) -> p c r", r=P)[:, :, : TOP - 1])
+            nc.tensor.transpose(banks[4][:, c * P : (c + 1) * P], gate_rows[:, c * P : (c + 1) * P], ident[:])
+        nc.scalar.copy(gate_cols[:], banks[4][:, : CHUNKS * P].rearrange("p (c r) -> p c r", r=P)[:, :, : TOP - 1])
 
         def gated(dst, hf, r, a, b):
             factor = gate_rest[r - 1][:, a:b] if r else gate_first[:, a:b]

@@ -27,7 +27,7 @@ X_CASTS = [(0, 0, 128, "vector"), (0, 128, 256, "vector"), (0, 256, 512, "scalar
 X_QUANT = 256
 W1_GROUPS = [(0, 2), (2, 4), (4, 6), (6, 8)]
 W3_GROUPS = [(0, 2), (2, 4), (4, 6), (6, 7), (7, 8)]
-W2_GROUPS = [(0, 6), (6, 8)]
+W2_GROUPS = [(0, 8)]
 GATHER_GROUPS = [(0, 1), (1, 2), (2, 3), (3, 4), (4, 6), (6, 8)]
 TURN_GROUPS = [(2, 4), (4, 6), (0, 2), (6, 7), (7, 8)]
 QUANT_GROUPS = [(2, 4), (4, 6), (0, 2), (6, 7), (7, 8)]
@@ -62,9 +62,7 @@ def tile_moe_ecr_glu_relu_kernel(
         w3 = [sb("w3_%d" % a, [P, b - a, 2 * H], U8) for a, b in W3_GROUPS]
         w2 = [sb("w2_%d" % a, [P, b - a, 2 * N], U8) for a, b in W2_GROUPS]
         gate_first = sb("gate_first", [P, T], F32)
-        gate_pair = sb("gate_pair", [P, 2, TV], F32)
-        gate_last = sb("gate_last", [P, TV], F32)
-        gate_rest = [gate_pair[:, 0, :], gate_pair[:, 1, :], gate_last[:]]
+        gate_rest = [sb("gate_rest%d" % r, [P, TV], F32) for r in range(1, TOP)]
         gate_rows = sb("gate_rows", [P, T - TV], F32)
         gate_cols = sb("gate_cols", [P, CHUNKS, TOP - 1], F32)
         ident = sb("ident", [P, P], F32)
@@ -118,12 +116,11 @@ def tile_moe_ecr_glu_relu_kernel(
         load_words(w1[3], w1_words, *W1_GROUPS[3])
         load_words(w3[4], w3_words, *W3_GROUPS[4])
         load_scales(nc.sync, s2, w2_scales, 0, E)
-        load_words(w2[0], w2_words, *W2_GROUPS[0])
         for r in (1, 2, 3):
             nc.sync.dma_start(pos_sb[r][:], (pos1, pos2, pos3, pos4)[r])
-        nc.sync.dma_start(out=gate_pair[:], in_=gate[1:3, 0:P, :TV].rearrange("r p t -> p r t"))
-        load_words(w2[1], w2_words, *W2_GROUPS[1])
-        nc.sync.dma_start(out=gate_last[:], in_=gate[3, 0:P, :TV])
+        load_words(w2[0], w2_words, *W2_GROUPS[0])
+        for r in (1, 2, 3):
+            nc.sync.dma_start(out=gate_rest[r - 1][:], in_=gate[r, 0:P, :TV])
         nc.sync.dma_start(out=gate_rows[0 : TOP - 1, :], in_=gate[1:TOP, 0, TV:T])
         nc.sync.dma_start(pos_sb[0][:], pos1)
         nc.sync.dma_start(out=gate_first[:], in_=gate[0, 0:P, :])

@@ -22,8 +22,8 @@ RELU = mybir.ActivationFunctionType.Relu
 COPY = mybir.ActivationFunctionType.Copy
 
 P = 128
-X_LOADS = [(0, 512), (512, 768)]
-X_CASTS = [(0, 0, 128, "vector"), (0, 128, 256, "vector"), (0, 256, 512, "scalar"), (1, 512, 680, "vector"), (1, 680, 768, "scalar")]
+X_LOADS = [(0, 512), (512, 640), (640, 768)]
+X_CASTS = [(0, 0, 256, "vector"), (0, 256, 352, "vector"), (0, 352, 512, "scalar"), (1, 512, 640, "scalar"), (2, 640, 768, "vector")]
 X_QUANT = 256
 W1_GROUPS = [(0, 2), (2, 4), (4, 6), (6, 8)]
 W3_GROUPS = [(0, 2), (2, 4), (4, 6), (6, 7), (7, 8)]
@@ -143,12 +143,12 @@ def tile_moe_ecr_glu_relu_kernel(
 
         for cast in X_CASTS[:3]:
             interleave(*cast)
-        quantise_x(0, 128)
-        quantise_x(128, 256)
+        quantise_x(0, 256)
+        quantise_x(256, 512)
         for cast in X_CASTS[3:]:
             interleave(*cast)
-        quantise_x(256, 512)
-        quantise_x(512, 768)
+        quantise_x(512, 640)
+        quantise_x(640, 768)
 
         def gather_tokens(a, b):
             lst = offs_sb[:, a * C // 16 : b * C // 16]

@@ -26,7 +26,7 @@ X_LOADS = [(0, 512), (512, 640), (640, 768)]
 X_CASTS = [(0, 0, 256, "vector"), (0, 256, 352, "vector"), (0, 352, 512, "scalar"), (1, 512, 640, "scalar"), (2, 640, 768, "vector")]
 X_QUANT = 256
 W1_GROUPS = [(0, 2), (2, 4), (4, 6), (6, 8)]
-W3_GROUPS = [(0, 2), (2, 4), (4, 6), (6, 7), (7, 8)]
+W3_GROUPS = W1_GROUPS
 W2_GROUPS = [(0, 8)]
 GATHER_GROUPS = [(0, 1), (1, 2), (2, 3), (3, 4), (4, 6), (6, 8)]
 TURN_GROUPS = [(2, 4), (4, 6), (0, 2), (6, 7), (7, 8)]
@@ -75,9 +75,9 @@ def tile_moe_ecr_glu_relu_kernel(
         y = [sb("y%d" % hf, [P, S + PAD], F32) for hf in range(2)]
 
         banks = [psum.tile([P, 512], F32, name="bank%d" % i) for i in range(8)]
-        bank_a = [banks[i] for i in (0, 1, 6, 7, 0, 1, 7, 4)]
-        bank_b = [banks[i] for i in (2, 3, 4, 5, 2, 3, 6, 5)]
-        bank_t = [banks[i] for i in (7, 4, 6, 0, 5)]
+        bank_a = [banks[i] for i in (0, 1, 6, 7, 0, 1, 7, 6)]
+        bank_b = [banks[i] for i in (2, 3, 4, 5, 2, 3, 4, 5)]
+        bank_t = [banks[i] for i in (7, 6, 4, 0, 5)]
 
         def zero(eng, t):
             eng.memset(t[:].rearrange("p e n -> p (e n)").bitcast(I32), 0)
@@ -110,11 +110,8 @@ def tile_moe_ecr_glu_relu_kernel(
         load_words(w1[0], w1_words, *W1_GROUPS[0])
         load_words(w1[1], w1_words, *W1_GROUPS[1])
         load_scales(nc.sync, s3, w3_scales, 0, E)
-        for w, src, g in ((w3, w3_words, 0), (w3, w3_words, 1), (w1, w1_words, 2), (w3, w3_words, 2)):
+        for w, src, g in ((w3, w3_words, 0), (w3, w3_words, 1), (w1, w1_words, 2), (w3, w3_words, 2), (w1, w1_words, 3), (w3, w3_words, 3)):
             load_words(w[g], src, *W1_GROUPS[g])
-        load_words(w3[3], w3_words, *W3_GROUPS[3])
-        load_words(w1[3], w1_words, *W1_GROUPS[3])
-        load_words(w3[4], w3_words, *W3_GROUPS[4])
         load_scales(nc.sync, s2, w2_scales, 0, E)
         for r in (1, 2, 3):
             nc.sync.dma_start(pos_sb[r][:], (pos1, pos2, pos3, pos4)[r])
@@ -249,10 +246,10 @@ def tile_moe_ecr_glu_relu_kernel(
         up_a(5)
         up_b(4)
         up_b(5)
-        up_b(6)
         up_a(6)
-        product(2)
         up_a(7)
+        product(2)
+        up_b(6)
         product(3)
         up_b(7)
         turn(0)
@@ -274,9 +271,9 @@ def tile_moe_ecr_glu_relu_kernel(
         quantise_h(4)
         results(0, 6, 7, banks[1], nc.vector.tensor_copy)
         results(0, 7, 8, banks[7], nc.vector.tensor_copy)
-        second_layer(1, (7, 6, 0, 1), banks[4])
+        second_layer(1, (7, 6, 0, 1), banks[6])
         nc.scalar.copy(
-            y[1][:, :S].rearrange("p (g c) -> p g c", c=2 * C)[:, 0:4:3, :], banks[4][:].rearrange("p (g c) -> p g c", c=2 * C)
+            y[1][:, :S].rearrange("p (g c) -> p g c", c=2 * C)[:, 0:4:3, :], banks[6][:].rearrange("p (g c) -> p g c", c=2 * C)
         )
         results(1, 2, 6, banks[7])
 
@@ -286,15 +283,15 @@ def tile_moe_ecr_glu_relu_kernel(
         def add_turned(dst, src, start, stop):
             nc.tensor.matmul(dst, src, ident[:], start=start, stop=stop, is_transpose=True)
 
-        sum_banks = [banks[5], banks[6]]
+        sum_banks = [banks[5], banks[4]]
         plain_banks = {1: banks[3], 2: banks[0], 3: banks[1]}
         back_banks = [banks[2], banks[2]]
         half = TV // 2
         turn_from = (0, half)
 
         for c in range(CHUNKS):
-            nc.tensor.transpose(banks[4][:, c * P : (c + 1) * P], gate_rows[:, c * P : (c + 1) * P], ident[:])
-        nc.scalar.copy(gate_cols[:], banks[4][:, : CHUNKS * P].rearrange("p (c r) -> p c r", r=P)[:, :, : TOP - 1])
+            nc.tensor.transpose(banks[6][:, c * P : (c + 1) * P], gate_rows[:, c * P : (c + 1) * P], ident[:])
+        nc.scalar.copy(gate_cols[:], banks[6][:, : CHUNKS * P].rearrange("p (c r) -> p c r", r=P)[:, :, : TOP - 1])
 
         def gated(dst, hf, r, a, b):
             factor = gate_rest[r - 1][:, a:b] if r else gate_first[:, a:b]

@@ -33,6 +33,7 @@ TURN_GROUPS = [(2, 4), (4, 6), (0, 2), (6, 7), (7, 8)]
 QUANT_GROUPS = [(2, 4), (4, 6), (0, 2), (6, 7), (7, 8)]
 POOL_EXPERTS = 2
 TV = 512
+ORDER = (3, 0, 1, 2)
 CHUNKS = (T - TV) // P
 
 
@@ -114,13 +115,13 @@ def tile_moe_ecr_glu_relu_kernel(
             load_words(w[g], src, *W1_GROUPS[g])
         load_scales(nc.sync, s2, w2_scales, 0, E)
         for r in (1, 2, 3):
-            nc.sync.dma_start(pos_sb[r][:], (pos1, pos2, pos3, pos4)[r])
+            nc.sync.dma_start(pos_sb[r][:], (pos1, pos2, pos3, pos4)[ORDER[r]])
         load_words(w2[0], w2_words, *W2_GROUPS[0])
         for r in (1, 2, 3):
-            nc.sync.dma_start(out=gate_rest[r - 1][:], in_=gate[r, 0:P, :TV])
-        nc.sync.dma_start(out=gate_rows[0 : TOP - 1, :], in_=gate[1:TOP, 0, TV:T])
-        nc.sync.dma_start(pos_sb[0][:], pos1)
-        nc.sync.dma_start(out=gate_first[:], in_=gate[0, 0:P, :])
+            nc.sync.dma_start(out=gate_rest[r - 1][:], in_=gate[ORDER[r], 0:P, :TV])
+        nc.sync.dma_start(out=gate_rows[0 : TOP - 1, :], in_=gate[0 : TOP - 1, 0, TV:T])
+        nc.sync.dma_start(pos_sb[0][:], pos4)
+        nc.sync.dma_start(out=gate_first[:], in_=gate[ORDER[0], 0:P, :])
 
         def interleave(c, a, b, engine):
             copy = nc.vector.tensor_copy if engine == "vector" else nc.scalar.copy
@@ -275,7 +276,7 @@ def tile_moe_ecr_glu_relu_kernel(
         nc.scalar.copy(
             y[1][:, :S].rearrange("p (g c) -> p g c", c=2 * C)[:, 0:4:3, :], banks[6][:].rearrange("p (g c) -> p g c", c=2 * C)
         )
-        results(1, 2, 6, banks[7])
+        results(1, 2, 6, banks[2])
 
         def offsets(r, a, b):
             return pos_sb[r][:, a // 16 : b // 16]

from contextlib import ExitStack

import concourse.mybir as mybir
from concourse.masks import make_identity

K, T, E, C, H, N = 512, 768, 8, 128, 512, 256
TOP, PAD = 4, 64
S = E * C
FLOPS = 2 * S * (2 * K * H + H * N)

F32 = mybir.dt.float32
BF16 = mybir.dt.bfloat16
I32 = mybir.dt.int32
U32 = mybir.dt.uint32
U16 = mybir.dt.uint16
U8 = mybir.dt.uint8
FP8X4 = mybir.dt.float8_e4m3fn_x4
FP4X4 = mybir.dt.float4_e2m1fn_x4
MULT = mybir.AluOpType.mult
ADD = mybir.AluOpType.add
RELU = mybir.ActivationFunctionType.Relu
COPY = mybir.ActivationFunctionType.Copy

P = 128
X_LOADS = [(0, 512), (512, 640), (640, 768)]
X_CASTS = [(0, 0, 256, "vector"), (0, 256, 352, "vector"), (0, 352, 512, "scalar"), (1, 512, 640, "scalar"), (2, 640, 768, "vector")]
X_QUANT = 256
W1_GROUPS = [(0, 2), (2, 4), (4, 6), (6, 8)]
W3_GROUPS = W1_GROUPS
W2_GROUPS = [(0, 8)]
GATHER_GROUPS = [(0, 1), (1, 2), (2, 3), (3, 4), (4, 6), (6, 8)]
TURN_GROUPS = [(2, 4), (4, 6), (0, 2), (6, 7), (7, 8)]
QUANT_GROUPS = [(2, 4), (4, 6), (0, 2), (6, 7), (7, 8)]
POOL_EXPERTS = 2
TV = 512
ORDER = (3, 0, 1, 2)
CHUNKS = (T - TV) // P


def tile_moe_ecr_glu_relu_kernel(
    tc, xT, w1_words, w1_scales, w3_words, w3_scales, w2_words, w2_scales, gate, offs, pos1, pos2, pos3, pos4, out
):
    nc = tc.nc
    with ExitStack() as ctx:
        keep = ctx.enter_context(tc.tile_pool(name="keep", bufs=1))
        psum = ctx.enter_context(tc.psum_pool(name="psum", bufs=1))

        def sb(name, shape, dtype, tag=None):
            return keep.tile(shape, dtype, name=name, tag=tag or name, align_bytes=64)

        offs_sb = sb("offs_sb", [P, S // 16], U16)
        pos_sb = [sb("pos_sb%d" % r, [P, T // 16], U16) for r in range(TOP)]
        x_raw = [sb("x_raw%d" % a, [P, 4, b - a], F32) for a, b in X_LOADS]
        x_bf = [sb("x_bf%d" % c, [P, X_QUANT, 4], BF16) for c in range(T // X_QUANT)]
        x_words = sb("x_words", [P, T], U32)
        x_scales = sb("x_scales", [P, T], U8)
        g_words = sb("g_words", [P, S], U32)
        g_scales = sb("g_scales", [P, S], U8)
        s1 = sb("s1", [P, E, H], U8)
        s3 = sb("s3", [P, E, H], U8)
        s2 = sb("s2", [P, E, N], U8)
        w1 = [sb("w1_%d" % a, [P, b - a, 2 * H], U8) for a, b in W1_GROUPS]
        w3 = [sb("w3_%d" % a, [P, b - a, 2 * H], U8) for a, b in W3_GROUPS]
        w2 = [sb("w2_%d" % a, [P, b - a, 2 * N], U8) for a, b in W2_GROUPS]
        gate_first = sb("gate_first", [P, T], F32)
        gate_rest = [sb("gate_rest%d" % r, [P, TV], F32) for r in range(1, TOP)]
        gate_rows = sb("gate_rows", [P, T - TV], F32)
        gate_cols = sb("gate_cols", [P, CHUNKS, TOP - 1], F32)
        ident = sb("ident", [P, P], F32)
        warm = sb("warm", [P, 8], F32)
        relu_a = [sb("relu_a%d" % e, [P, H], F32) for e in range(E)]
        gate_b = [sb("gate_b%d" % e, [P, H], F32) for e in range(POOL_EXPERTS)]
        h_rows = {e: sb("h_rows%d" % e, [P, H], BF16) for e in range(POOL_EXPERTS, E)}
        h_cols = [sb("h_cols%d" % a, [P, (b - a) * H], BF16) for a, b in QUANT_GROUPS]
        h_scales = [sb("h_scales%d" % a, [P, (b - a) * C], U8) for a, b in QUANT_GROUPS]
        y = [sb("y%d" % hf, [P, S + PAD], F32) for hf in range(2)]

        banks = [psum.tile([P, 512], F32, name="bank%d" % i) for i in range(8)]
        bank_a = [banks[i] for i in (0, 1, 6, 7, 0, 1, 7, 6)]
        bank_b = [banks[i] for i in (2, 3, 4, 5, 2, 3, 4, 5)]
        bank_t = [banks[i] for i in (7, 6, 4, 0, 5)]

        def zero(eng, t):
            eng.memset(t[:].rearrange("p e n -> p (e n)").bitcast(I32), 0)

        def load_scales(eng, plane, src, a, b):
            for r in range(4):
                eng.dma_start(
                    out=plane[r:P:32, :, :].bitcast(I32),
                    in_=src[a:b, 0, r:16:4, :].rearrange("e q n -> q e n").bitcast(I32),
                )

        def load_words(dst, src, a, b):
            nc.sync.dma_start(out=dst[:].bitcast(I32), in_=src[a:b, 0].rearrange("e p n -> p e n").bitcast(I32))

        zero(nc.vector, s1)
        zero(nc.gpsimd, s3)
        make_identity(nc, ident[:])
        nc.gpsimd.memset(gate_rows[:], 0.0)
        zero(nc.vector, s2)
        nc.vector.memset(x_scales[:].bitcast(I32), 0)
        for hf in range(2):
            nc.vector.memset(y[hf][:, S:], 0.0)
        nc.vector.memset(warm[:, 0:4], 0.0)
        nc.scalar.activation(warm[:, 4:8], warm[:, 0:4], RELU)

        for c, (a, b) in enumerate(X_LOADS):
            nc.sync.dma_start(out=x_raw[c][:], in_=xT[:, a:b].rearrange("(p j) w -> p j w", j=4))
        nc.sync.dma_start(offs_sb[:], offs)
        load_scales(nc.sync, s1, w1_scales, 0, E)
        load_words(w1[0], w1_words, *W1_GROUPS[0])
        load_words(w1[1], w1_words, *W1_GROUPS[1])
        load_scales(nc.sync, s3, w3_scales, 0, E)
        for w, src, g in ((w3, w3_words, 0), (w3, w3_words, 1), (w1, w1_words, 2), (w3, w3_words, 2), (w1, w1_words, 3), (w3, w3_words, 3)):
            load_words(w[g], src, *W1_GROUPS[g])
        load_scales(nc.sync, s2, w2_scales, 0, E)
        for r in (1, 2, 3):
            nc.sync.dma_start(pos_sb[r][:], (pos1, pos2, pos3, pos4)[ORDER[r]])
        load_words(w2[0], w2_words, *W2_GROUPS[0])
        for r in (1, 2, 3):
            nc.sync.dma_start(out=gate_rest[r - 1][:], in_=gate[ORDER[r], 0:P, :TV])
        nc.sync.dma_start(out=gate_rows[0 : TOP - 1, :], in_=gate[0 : TOP - 1, 0, TV:T])
        nc.sync.dma_start(pos_sb[0][:], pos4)
        nc.sync.dma_start(out=gate_first[:], in_=gate[ORDER[0], 0:P, :])

        def interleave(c, a, b, engine):
            copy = nc.vector.tensor_copy if engine == "vector" else nc.scalar.copy
            q, first = a // X_QUANT, X_LOADS[c][0]
            copy(
                x_bf[q][:, a - q * X_QUANT : b - q * X_QUANT, :].rearrange("p (c i) t -> p c t i", i=4),
                x_raw[c][:, :, a - first : b - first].rearrange("p t (c i) -> p c t i", i=4),
            )

        def quantise_x(a, b):
            q = a // X_QUANT
            nc.vector.quantize_mx(
                out=x_words[:, a:b].bitcast(FP8X4),
                scales=x_scales[:, a:b],
                in_=x_bf[q][:, a - q * X_QUANT : b - q * X_QUANT, :].rearrange("p w t -> p (w t)"),
            )

        for cast in X_CASTS[:3]:
            interleave(*cast)
        quantise_x(0, 256)
        quantise_x(256, 512)
        for cast in X_CASTS[3:]:
            interleave(*cast)
        quantise_x(512, 640)
        quantise_x(640, 768)

        def gather_tokens(a, b):
            lst = offs_sb[:, a * C // 16 : b * C // 16]
            nc.vector.tensor_copy(g_scales[:, a * C : b * C], x_scales[:].indirect(lst))
            nc.vector.tensor_copy(g_words[:, a * C : b * C], x_words[:].indirect(lst))

        def group_of(groups, e):
            return [i for i, (a, b) in enumerate(groups) if a <= e < b][0]

        def first_layer(e, bank, w, s, groups):
            g = group_of(groups, e)
            cols = slice(e * C, (e + 1) * C)
            nc.tensor.matmul_mx(
                out=bank[:],
                lhsT=g_words[:, cols].bitcast(FP8X4),
                lhsT_scale=g_scales[:, cols],
                rhs=w[g][:, e - groups[g][0], :].bitcast(FP4X4),
                rhs_scale=s[:, e, :],
                start=True,
                stop=True,
            )

        def up_a(e):
            first_layer(e, bank_a[e], w1, s1, W1_GROUPS)
            relu(e)

        def up_b(e):
            first_layer(e, bank_b[e], w3, s3, W3_GROUPS)

        def by_word(ap):
            return ap.rearrange("s (m u d) -> s u m d", u=2, d=2)

        def in_order(ap):
            return ap.rearrange("s (u m d) -> s u m d", u=2, d=2)

        def relu(e):
            nc.scalar.activation(in_order(relu_a[e][:]), by_word(bank_a[e][:]), RELU)

        def product(e):
            nc.vector.tensor_tensor(in_order(h_rows[e][:]), by_word(bank_b[e][:]), in_order(relu_a[e][:]), MULT)

        def turn(g, copy=nc.scalar.copy):
            a, b = TURN_GROUPS[g]
            bank = bank_t[g]
            for e in range(a, b):
                words = h_rows[e][:, :].bitcast(F32)
                for u in range(2):
                    c = (2 * (e - a) + u) * P
                    nc.tensor.transpose(bank[:, c : c + P], words[:, u * P : (u + 1) * P], ident[:])
            q = group_of(QUANT_GROUPS, a)
            first_col = (a - QUANT_GROUPS[q][0]) * H
            copy(
                h_cols[q][:, first_col : first_col + (b - a) * H].bitcast(F32).rearrange("p (e s u) -> p e s u", u=2, s=C),
                bank[:, : (b - a) * 2 * P].rearrange("p (e u s) -> p e s u", u=2, s=C),
            )

        def quantise_h(q):
            a, b = QUANT_GROUPS[q]
            nc.vector.quantize_mx(
                out=h_words[:, a * C : b * C].bitcast(FP8X4),
                scales=h_scales[q][:],
                in_=h_cols[q][:],
            )

        def second_layer(hf, experts, bank):
            for e in experts:
                n = sorted(experts).index(e)
                q, g = group_of(QUANT_GROUPS, e), group_of(W2_GROUPS, e)
                cols = slice((e - QUANT_GROUPS[q][0]) * C, (e - QUANT_GROUPS[q][0] + 1) * C)
                nc.tensor.matmul_mx(
                    out=bank[:, n * C : (n + 1) * C],
                    lhsT=w2[g][:, e - W2_GROUPS[g][0], hf * 2 * P : (hf + 1) * 2 * P].bitcast(FP4X4),
                    lhsT_scale=s2[:, e, hf * P : (hf + 1) * P],
                    rhs=h_words[:, e * C : (e + 1) * C].bitcast(FP8X4),
                    rhs_scale=h_scales[q][:, cols],
                    start=True,
                    stop=True,
                )

        def results(hf, a, b, bank, copy=nc.scalar.copy):
            second_layer(hf, range(a, b), bank)
            copy(y[hf][:, a * C : b * C], bank[:, : (b - a) * C])

        for a, b in GATHER_GROUPS:
            gather_tokens(a, b)
        pool_rows = sb("pool_rows", [P, POOL_EXPERTS, H], BF16, "x_words")
        for e in range(POOL_EXPERTS):
            h_rows[e] = pool_rows[:, e, :]
        for e in range(4):
            up_a(e)
        for e in range(POOL_EXPERTS):
            up_b(e)
            nc.scalar.copy(in_order(gate_b[e][:]), by_word(bank_b[e][:]))
            nc.gpsimd.tensor_tensor(h_rows[e], gate_b[e][:], relu_a[e][:], MULT)
        up_b(2)
        up_b(3)
        up_a(4)
        up_a(5)
        up_b(4)
        up_b(5)
        up_a(6)
        up_a(7)
        product(2)
        up_b(6)
        product(3)
        up_b(7)
        turn(0)
        product(4)
        product(5)
        turn(1)
        product(6)
        product(7)
        h_words = sb("h_words", [P, S], U32, "relu_a7")
        turn(2)
        quantise_h(0)
        quantise_h(1)
        turn(3)
        turn(4, nc.vector.tensor_copy)
        results(0, 2, 6, banks[2])
        quantise_h(2)
        results(0, 0, 2, banks[3])
        quantise_h(3)
        quantise_h(4)
        results(0, 6, 7, banks[1], nc.vector.tensor_copy)
        results(0, 7, 8, banks[7], nc.vector.tensor_copy)
        second_layer(1, (7, 6, 0, 1), banks[6])
        nc.scalar.copy(
            y[1][:, :S].rearrange("p (g c) -> p g c", c=2 * C)[:, 0:4:3, :], banks[6][:].rearrange("p (g c) -> p g c", c=2 * C)
        )
        results(1, 2, 6, banks[2])

        def offsets(r, a, b):
            return pos_sb[r][:, a // 16 : b // 16]

        def add_turned(dst, src, start, stop):
            nc.tensor.matmul(dst, src, ident[:], start=start, stop=stop, is_transpose=True)

        sum_banks = [banks[5], banks[4]]
        plain_banks = {1: banks[3], 2: banks[0], 3: banks[1]}
        back_banks = [banks[2], banks[2]]
        half = TV // 2
        turn_from = (0, half)

        for c in range(CHUNKS):
            nc.tensor.transpose(banks[6][:, c * P : (c + 1) * P], gate_rows[:, c * P : (c + 1) * P], ident[:])
        nc.scalar.copy(gate_cols[:], banks[6][:, : CHUNKS * P].rearrange("p (c r) -> p c r", r=P)[:, :, : TOP - 1])

        def gated(dst, hf, r, a, b):
            factor = gate_rest[r - 1][:, a:b] if r else gate_first[:, a:b]
            nc.vector.tensor_tensor(dst, y[hf][:].indirect(offsets(r, a, b)), factor, MULT)

        def gated_term(hf, r):
            prod = sb("prod%d%d" % (hf, r), [P, TV], F32, None)
            gated(prod[:], hf, r, 0, TV)
            for c in range(turn_from[hf], TV, P):
                add_turned(
                    sum_banks[hf][:, c : c + P], prod[:, c : c + P], r == 1 and c == turn_from[hf], r == TOP - 1 and c == TV - P
                )
            return prod

        def gated_back(hf):
            turned = sb("turned%d" % hf, [P, TV], F32)
            nc.scalar.copy(turned[:, turn_from[hf] :], sum_banks[hf][:, turn_from[hf] :])
            for c in range(turn_from[hf], TV, P):
                nc.tensor.transpose(sum_banks[hf][:, c : c + P], turned[:, c : c + P], ident[:])

        def plain_fetch(hf, r):
            got = sb("plain%d%d" % (hf, r), [P, T - TV], F32)
            nc.scalar.activation(got[:], y[hf][:].indirect(offsets(r, TV, T)), COPY)
            for c in range(CHUNKS):
                col = (2 * c + hf) * P
                nc.tensor.transpose(plain_banks[r][:, col : col + P], got[:, c * P : (c + 1) * P], ident[:])

        def plain_back(r):
            scaled = sb("scaled%d" % r, [P, CHUNKS, 2 * P], F32)
            for c in range(CHUNKS):
                factor = gate_cols[:, c, r - 1 : r]
                nc.scalar.activation(scaled[:, c, :], plain_banks[r][:, 2 * c * P : 2 * (c + 1) * P], COPY, scale=factor)
                for hf in range(2):
                    add_turned(
                        back_banks[c][:, (hf * CHUNKS + c) * P : (hf * CHUNKS + c + 1) * P],
                        scaled[:, c, hf * P : (hf + 1) * P],
                        r == 1 and hf == 0 and c == 0,
                        r == TOP - 1 and hf == 1 and c == CHUNKS - 1,
                    )

        first = sb("first", [P, 2, T], F32)

        def close(name, rows, a, b, src0, src1):
            res = sb(name, [P, b - a], F32)
            nc.vector.tensor_tensor(res[:], src0, src1, ADD)
            nc.sync.dma_start(out=out[rows, a:b], in_=res[:])

        def close_plain(hf):
            w = T - TV
            close("res_s%d" % hf, slice(hf * P, (hf + 1) * P), TV, T, back_banks[0][:, hf * w : (hf + 1) * w], first[:, hf, TV:])

        gated_term(0, 1)
        plain_fetch(0, 1)
        gated_term(0, 2)
        plain_fetch(1, 1)
        gated_term(0, 3)
        plain_fetch(0, 2)
        p1 = gated_term(1, 1)
        gated_back(0)
        plain_fetch(1, 2)
        p2 = gated_term(1, 2)
        plain_back(1)
        p3 = gated_term(1, 3)
        plain_fetch(0, 3)
        gated(first[:, 0, :TV], 0, 0, 0, TV)
        plain_fetch(1, 3)
        sum12 = sb("sum12", [P, half], F32)
        nc.vector.tensor_tensor(sum12[:], p1[:, :half], p2[:, :half], ADD)
        close("res0", slice(0, P), 0, TV, sum_banks[0][:], first[:, 0, :TV])
        gated_back(1)
        plain_back(2)
        gated(first[:, 1, :TV], 1, 0, 0, TV)
        plain_back(3)
        gated(first[:, 0, TV:], 0, 0, TV, T)
        nc.vector.tensor_tensor(p3[:, :half], p3[:, :half], first[:, 1, :half], ADD)
        close("res1", slice(P, 2 * P), half, TV, sum_banks[1][:, half:], first[:, 1, half:TV])
        close("res2", slice(P, 2 * P), 0, half, sum12[:], p3[:, :half])
        gated(first[:, 1, TV:], 1, 0, TV, T)
        close_plain(0)
        close_plain(1)
